import numpy as np, ml_dtypes
CORES = [35,38,43,46]
N = 4
BF = ml_dtypes.bfloat16
H, P, B, T, S = 4096, 1024, 256, 4, 32
BOUND = P + B * (np.arange(T * B) // B)
def parts(rng):
    G = P + T * B
    fe = (256 * (0.6 * rng.random((N, 8, 16, G)) + 0.4 * rng.random((N, 8, 1, G)))).astype(np.int64)
    no = (256 * (0.6 * rng.random((N, 8, 16, H)) + 0.4 * rng.random((N, 8, 1, H)))).astype(np.int64)
    no = np.minimum(no + rng.integers(0, 64, (N, 8, 1, 1)), 255)
    co = rng.integers(0, BOUND, (N, 8, 16, T * B))
    pool = np.argsort(rng.random((N, 8, H)), axis=-1)[..., :256]; ix = (256 * rng.random((N, 8, P)) ** 3).astype(np.int64)
    hv = np.where(rng.random((N, 8, P)) < 0.3, rng.integers(0, H, (N, 8, P)), np.take_along_axis(pool, ix, 2))
    return fe, no, co, hv
def pack(fe, no, co, hv):
    return {"lim": np.ascontiguousarray(no.reshape(N, 128, H)).astype(np.float32).astype(BF), "feat": np.ascontiguousarray(fe.reshape(N, 128, P + T * B)).astype(np.float32).astype(BF),
            "comp": np.ascontiguousarray(co.reshape(N, 128, T * B)).astype(np.int32), "hd": np.ascontiguousarray(hv).astype(np.int32)}
def setup_inputs(rng):
    return pack(*parts(rng))
def setup_inputs_ties(rng):
    fe, no, co, hv = parts(rng)
    d = rng.permutation(np.array([1, 2, S - 1, S, S + 1, S, 1, S + 1])).reshape(1, 8, 1, 1)
    fe = 100 + d * (rng.random(fe.shape) < 0.8).astype(np.int64); no = 100 + d * (rng.random(no.shape) < 0.35).astype(np.int64)
    fe[..., 1::2] = fe[..., 0::2].copy()
    co[:, :, 8:, ::3] = co[:, :, :8, ::3].copy()
    return pack(fe, no, co, hv)
def setup_inputs_alike(rng):
    fe, no, co, hv = parts(rng)
    hv[:, ::2] = rng.choice(np.array([0, H - 1, H // 2, 37]), (N, 4, P)); hv[..., 0] = H - 1; hv[..., P - 1] = 0
    no[:, :4] = rng.integers(200, 256, (N, 4, 16, H))
    co[:, 1] = co[:, 1, :1].copy()
    co[:, 3] = np.where(rng.random((N, 16, T * B)) < 0.5, 0, BOUND - 1)
    co[:, 5] = rng.integers(BOUND - B, BOUND, (N, 16, T * B))
    co[:, 7, 2:] = np.where(rng.random((N, 14, T * B)) < 0.5, co[:, 7, :1], co[:, 7, 1:2])
    return pack(fe, no, co, hv)
def setup_inputs_ends(rng):
    fe, no, co, hv = parts(rng); M = T * B; k = np.arange(16)[:, None]
    for g in range(5): hv[:, g] = rng.permutation(H)[:P]
    no[:, :5] = 255
    o = np.argsort(rng.random((N, 16, M)), axis=1); s = rng.integers(0, P // 2, (N, 1, M))
    fe[:, 0] = 255; fe[:, 0, :, 1:P:2] = 0
    co[:, 0] = np.where(o < 2, 2 * rng.integers(0, P // 2, (N, 1, M)) + 1, 2 * ((s + o) % (P // 2)))
    fe[:, 1, :, :P] = rng.integers(200, 256, (N, 16, P)); fe[:, 1, :, P:] = 255
    lo = np.argsort(rng.random((N, 3, T, B)), axis=-1)
    lo[:, 1:] = 0; lo[:, 2, :, 1:-1] = 1 + np.argsort(rng.random((N, T, B - 1)), axis=-1)[..., :B - 2]
    w = B + rng.integers(0, P - B, (N, 3, 1, M))
    co[:, 2:5] = np.where(k == rng.integers(0, 16, (N, 3, 1, M)), lo.reshape(N, 3, 1, M), w)
    fe[:, 2:5, :, P:] = rng.integers(0, 160, (N, 3, 16, M)); fe[:, 4, :, P::B] = 255
    for g, b in ((5, 254), (6, 0)):
        fe[:, g] = b + (rng.random((N, 16, P + M)) < 0.8).astype(np.int64); no[:, g] = b + (rng.random((N, 16, H)) < 0.3).astype(np.int64)
    return pack(fe, no, co, hv)
def setup_inputs_still(rng):
    fe, no, co, hv = parts(rng); fe = np.maximum(fe, 1)
    z = rng.integers(0, 3, (N, 8, 1, 1)); z[:, 0] = 0; z[:, 1] = 1; z[:, 2] = 2
    return pack(fe, np.where(z == 0, 255, np.where(z == 1, 0, no)), co, hv)
def setup_inputs_spread(rng):
    fe, no, co, hv = parts(rng)
    fe = (np.exp2(8 * rng.random((N, 8, 1, P + T * B))) * rng.random(fe.shape)).astype(np.int64)
    no = (np.exp2(8 * rng.random((N, 8, 1, H))) * rng.random(no.shape)).astype(np.int64)
    hv = (H * rng.random((N, 8, P)) ** 4).astype(np.int64)
    return pack(fe, no, co, hv)
def check_inputs(d):
    bad = []
    for k in ("lim", "feat"):
        x = np.asarray(d[k]).astype(np.float32)
        if not np.all((x >= 0) & (x <= 255) & (x == np.floor(x))): bad.append("whole numbers of " + k)
    if np.min(d["hd"]) < 0 or np.max(d["hd"]) > H - 1: bad.append("range of hd")
    if np.min(d["comp"]) < 0 or not np.all(np.asarray(d["comp"]) < BOUND): bad.append("range of comp")
    return bad
def reference(lim, feat, comp, hd):
    fe = feat.astype(np.float32).astype(np.int16).reshape(N, 8, 16, P + T * B); no = lim.astype(np.float32).astype(np.int16).reshape(N, 8, 16, H)
    co = comp.astype(np.int64).reshape(N, 8, 16, T * B)
    h = np.zeros((N, 8, P + T * B), np.int64); h[:, :, :P] = hd
    kappa = np.zeros(N, np.int64); ranks = np.arange(N)
    for t in range(T):
        fv = fe[..., P + t * B:P + (t + 1) * B]
        ix = co[..., t * B:(t + 1) * B].reshape(N, 8, 16 * B)
        c = np.take_along_axis(h, ix, 2)
        fc = np.take_along_axis(fe, ix[:, :, None, :], 3).reshape(N, 8, 16, 16, B)
        share = np.add.reduce(np.minimum(fv[:, :, :, None, :], fc), axis=2, dtype=np.int64)
        for a in range(N):
            q = (ranks + a) % N
            x = np.take_along_axis(no[q], c[:, :, None, :], 3).reshape(N, 8, 16, 16, B)
            n = np.add.reduce(fv[:, :, :, None, :] > x, axis=2, dtype=np.int64).reshape(N, 8, 16 * B)
            c = np.where(n >= 9, ((c * c >> 5) + c + 613 * n + kappa[q][:, None, None]) & (H - 1), c)
        c = c.reshape(N, 8, 16, B)
        m = np.add.reduce(c[:, :, :, None, :] == c[:, :, None, :, :], axis=3, dtype=np.int64)
        key = 4096 * m + share
        won = np.take_along_axis(c, np.argmax(key, axis=2)[:, :, None, :], 2)[:, :, 0]
        lost = np.take_along_axis(c, np.argmin(key, axis=2)[:, :, None, :], 2)[:, :, 0]
        h[:, :, P + t * B:P + (t + 1) * B] = won
        for r in range(N):
            for g in range(8):
                e, first = np.unique(lost[r, g], return_index=True)
                old = no[r, g][:, e]
                no[r, g][:, e] = old + np.clip(fv[r, g][:, first] - old, -S, S)
        kappa = np.add.reduce(won, axis=(1, 2)) & 255
    return {"yh": h[:, :, P:].astype(np.float32), "yl": no.reshape(N, 128, H).astype(np.float32).astype(BF)}

@@ -1,0 +1,652 @@
+from concourse.bass import DstId, RemoteDMATransfer
+from concourse.mybir import AluOpType as A, ActivationFunctionType as F
+
+NR, RT, H, DUMMY, HALF = 4, 4, 4096, 256, 2048
+MOD = 131072
+KS = 130
+SLOPE = 613 * 32 + MOD * KS
+OFF = MOD * 512
+BV = -256 - MOD * (9 * KS + 1) - OFF
+BS = BV + 8 * SLOPE
+CHUNKS = ((0, 5, "V"), (5, 4, "S"), (9, 4, "V"), (13, 3, "S"))
+SHARE0 = (0, 2)
+CYC, GC, PEC = 0.83e-3 * 1.25, 1.56, 0.68e-3
+LOOK, LSAME, LCROSS = 0.3, 0.0, 0.0
+
+SCRATCH = {}
+SEMAPHORES = ["cv", "cs", "cp", "cg", "lsend"] + ["d%d" % j for j in range(52)] + ["ls%d" % j for j in range(10)]
+
+
+def _buf(names, cols, dtype, where="sbuf", rows=128):
+    for n in names.split():
+        SCRATCH[n] = (where, [rows] + (cols if isinstance(cols, list) else [cols]), dtype)
+
+
+B16, F32, I32, U16 = "bfloat16", "float32", "int32", "uint16"
+_buf("NB0 NB1 NB2 NB3", H + DUMMY, B16)
+_buf("FE HT", 2048, B16)
+_buf("FVT0 FVT1 FVT2 FVT3 XV0 XV1 XV2 XV3", 1280, B16)
+_buf("OUTV0 OUTV1 OUTV2 OUTV3", 264, B16)
+_buf("OUTL0 OUTL1 OUTL2 OUTL3 LU", 16, U16)
+for _t in range(RT - 1):
+    for _a in range(NR):
+        SEMAPHORES += ["iv%d_%d" % (_a, _t), "il%d_%d" % (_a, _t)]
+        if _a:
+            _buf("INV%d_%d" % (_a, _t), 264, B16)
+            _buf("INL%d_%d" % (_a, _t), 16, U16)
+for _a in range(1, NR):
+    SEMAPHORES += ["n%d_0" % _a, "n%d_1" % _a]
+_buf("ZL ZR", [32, 16], I32)
+_buf("Z ZT", [32, 32], I32)
+_buf("LT", 1024, U16)
+_buf("HD SPI", 64, I32)
+_buf("HDI", 128, I32)
+_buf("HDB BMW ID IDN IDK ONES", 128, B16)
+_buf("RI", 160, F32)
+_buf("RG", 128, F32)
+_buf("PI PM PG KI KJ", 2, I32)
+_buf("PF", 8, F32)
+_buf("MK DUP KV KW LF DL OF", 16, F32)
+_buf("MB", 160, B16)
+_buf("MIP", 16 * 160, B16)
+_buf("BI", 16 * 128, B16)
+_buf("E1 E05 ES1 ES5 ESN EX", 144, B16)
+_buf("ZERO FL OLD DC", 256, B16)
+_buf("TW C32 SQ M1", 256, F32)
+_buf("TRI", [16, 16], B16)
+_buf("GS0 GS1 GS2 GS3 SS0 SS1 SS2 SS3 XH0 XH1 GH0 GH1 SH0 SH1", 1024, B16)
+_buf("CL0 CL1 LB", 256, U16)
+_buf("TI CI", 256, I32)
+_buf("CW", 384, F32)
+_buf("EQ", [9, 256], B16)
+_buf("EQT", [16, 256], B16)
+_buf("KK DD", 512, F32)
+_buf("M2", 128, F32)
+_buf("M3", 64, F32)
+_buf("WLI", 32, I32)
+_buf("SPB", 64, B16)
+_buf("KS1", 2, F32)
+_buf("JUNK", 32, F32)
+_buf("YH8", 1024, F32, rows=8)
+_buf("B0 B1 B2 B3 B4 B5 KEY0 KEY1", 512, F32, "psum")
+PSUM = set(n for n in SCRATCH if SCRATCH[n][0] == "psum")
+CSEM = {"V": "cv", "S": "cs", "P": "cp", "G": "cg"}
+
+
+def add(gr, eng, emit, cost, reads=(), writes=(), kind="c", sem=None, val=0, lat=0.0, est=0.0, soft=()):
+    nodes = gr["nodes"]
+    i = len(nodes)
+    deps = set()
+    for w, regs in ((0, reads), (1, writes)):
+        for (b, c0, c1) in regs:
+            if b in PSUM:
+                st = gr["bank"].setdefault(b, [[], [], None])
+                if st[2] != eng:
+                    st[0], st[1], st[2] = st[1], [], eng
+                deps.update(e[0] for e in st[0])
+                deps.update(j for (j, d0, d1, dw) in st[1] if d0 < c1 and c0 < d1 and (w or dw))
+                st[1].append((i, c0, c1, w))
+            else:
+                keep = []
+                for e in gr["acc"].get(b, []):
+                    j, d0, d1, dw = e
+                    if d0 < c1 and c0 < d1 and (w or dw):
+                        deps.add(j)
+                    if not (w and j != i and c0 <= d0 and d1 <= c1):
+                        keep.append(e)
+                gr["acc"][b] = keep + [(i, c0, c1, w)]
+    deps.discard(i)
+    nodes.append({"id": i, "eng": eng, "emit": emit, "cost": cost, "kind": kind, "sem": sem, "val": val, "deps": deps,
+                  "soft": set(soft) - deps, "lat": lat, "est": est, "done": (sem, val)})
+    return i
+
+
+def schedule(gr):
+    nodes = gr["nodes"]
+    succ = [[] for _ in nodes]
+    for n in nodes:
+        for j in n["deps"] | n["soft"]:
+            succ[j].append(n["id"])
+    rank = [0.0] * len(nodes)
+    for n in reversed(nodes):
+        rank[n["id"]] = max([0.0] + [rank[s] for s in succ[n["id"]]]) + n["cost"] + n["lat"] + 0.05
+    left = [len(n["deps"] | n["soft"]) for n in nodes]
+    at = [n["est"] for n in nodes]
+    free, ready = {"R": 0.0}, {}
+    for n in nodes:
+        free[n["eng"]] = 0.0
+        ready.setdefault(n["eng"], set())
+        if left[n["id"]] == 0:
+            ready[n["eng"]].add(n["id"])
+    order = []
+    while len(order) < len(nodes):
+        best = None
+        for e in ready:
+            if ready[e]:
+                s = max(free[e], min(at[i] for i in ready[e]))
+                if best is None or s < best[0]:
+                    best = (s, e)
+        s, e = best
+        i = max((k for k in ready[e] if at[k] <= s), key=lambda k: (rank[k], -k))
+        if nodes[i]["cost"] > 0.4:
+            for k in sorted(ready[e]):
+                if at[k] <= s + LOOK * nodes[i]["cost"] and rank[k] > rank[i]:
+                    i = k
+        n = nodes[i]
+        s = max(free[e], at[i])
+        ready[e].discard(i)
+        if e != "R":
+            free[e] = s + n["cost"]
+        order.append(i)
+        for k in succ[i]:
+            left[k] -= 1
+            f = s + n["cost"]
+            if i in nodes[k]["deps"]:
+                f += n["lat"] + (LSAME if nodes[k]["eng"] == e else LCROSS)
+            at[k] = max(at[k], f)
+            if left[k] == 0:
+                ready[nodes[k]["eng"]].add(k)
+    return order
+
+
+def emit_all(gr, order, g, T):
+    q = {"V": g.vector, "S": g.scalar, "P": g.tensor, "G": g, "Y": g.sync}
+    nodes, clk = gr["nodes"], {}
+    known = dict((e, {}) for e in q)
+    final = {}
+    for i in order:
+        n = nodes[i]
+        if n["kind"] == "r":
+            final[n["sem"]] = n["val"]
+            continue
+        e = n["eng"]
+        cl = dict(known[e])
+        need = {}
+        for j in n["deps"]:
+            d = nodes[j]
+            if not (e == "P" and d["eng"] == "P"):
+                s, v = d["done"]
+                need[s] = max(need.get(s, 0), v)
+        items = sorted(need.items(), key=lambda x: (-x[1], x[0]))
+        for s, v in items:
+            if cl.get(s, 0) >= v or any(s2 != s and clk.get((s2, v2), {}).get(s, 0) >= v and known[e].get(s2, 0) < v2
+                                        for s2, v2 in items):
+                continue
+            q[e].wait_ge(T.sem[s], int(v))
+            cl[s] = v
+            for s3, v3 in clk.get((s, v), {}).items():
+                cl[s3] = max(cl.get(s3, 0), v3)
+        known[e] = cl
+        ins = n["emit"](q[e])
+        if n["kind"] == "c":
+            s = CSEM[e]
+            n["done"] = (s, final.get(s, 0) + 1)
+            ins.then_inc(T.sem[s], 1)
+        elif n["kind"] == "d":
+            ins.then_inc(T.sem[n["sem"]], 16)
+        final[n["done"][0]] = max(final.get(n["done"][0], 0), n["done"][1])
+        clk[n["done"]] = cl
+    for s in sorted(final):
+        if known["G"].get(s, 0) < final[s]:
+            g.wait_ge(T.sem[s], int(final[s]))
+
+
+def build(core, T, topo):
+    rank = T.rank_of(core)
+    gr = {"nodes": [], "acc": {}, "bank": {}}
+    num = {"d": 0, "ls": 0, "x": 0, "s": 0, "b": 0, "lsend": 0}
+    lastd = {}
+
+    def nxt(k, n):
+        num[k] += 1
+        return (num[k] - 1) % n
+
+    def W(n):
+        return (n, 0, 1 << 20)
+
+    def vec(fn, cyc, reads, writes):
+        return add(gr, "V", fn, max(64, cyc) * CYC + 0.02, reads, writes)
+
+    def gps(fn, cyc, writes):
+        return add(gr, "G", fn, cyc * CYC + 0.15, [], writes)
+
+    def dma(eng, out, in_, lat, reads, writes, soft=()):
+        s = "d%d" % nxt("d", 99)
+        lastd[eng] = add(gr, eng, lambda q: q.dma_start(out, in_), 0.06, reads, writes, "d", s, 16, lat,
+                         soft=list(soft) + ([lastd[eng]] if eng in lastd else []))
+
+    def tt(out, in0, in1, op, cyc, reads, writes):
+        return vec(lambda q: q.tensor_tensor(out=out, in0=in0, in1=in1, op=op), cyc, reads, writes)
+
+    def ts(out, in0, s1, op0, cyc, reads, writes, s2=None, op1=None):
+        if op1 is None:
+            return vec(lambda q: q.tensor_scalar(out=out, in0=in0, scalar1=s1, scalar2=None, op0=op0), cyc, reads, writes)
+        return vec(lambda q: q.tensor_scalar(out=out, in0=in0, scalar1=s1, scalar2=s2, op0=op0, op1=op1), cyc, reads, writes)
+
+    def cp(out, in_, cyc, reads, writes):
+        return vec(lambda q: q.tensor_copy(out=out, in_=in_), cyc, reads, writes)
+
+    def fill(ap, val, n, reg):
+        vec(lambda q: q.memset(ap, val), n, [], [reg])
+
+    def act(out, in_, func, cyc, reads, writes, bias=0.0, scale=1.0, accum=None, soft=()):
+        def f(q):
+            if accum is not None:
+                return q.activation(out=out, in_=in_, func=func, bias=bias, scale=scale, accum_out=accum)
+            return q.activation(out=out, in_=in_, func=func, bias=bias, scale=scale)
+        return add(gr, "S", f, max(64, cyc) * CYC + 0.04, reads, writes, soft=soft)
+
+    def mms(lst, reads, writes):
+        def f(q):
+            for (o, l, r, st, sp, _) in lst:
+                ins = q.matmul(o, l, r, st, sp)
+            return ins
+        return add(gr, "P", f, sum(max(64, x[5]) for x in lst) * PEC + 0.03, reads, writes)
+
+    def extract(bank, c0, parts, start, stop, n=64):
+        lst = []
+        for en, x in parts:
+            for i in range(16):
+                lst.append((T[bank][:, c0:c0 + n], T[en][:, 15 - i:143 - i], T[x][:, i:16 * n:16],
+                            start and not lst, stop and len(lst) == 16 * len(parts) - 1, n))
+        return mms(lst, [(x, 0, 16 * n) for _, x in parts] + [W(en) for en, _ in parts], [(bank, c0, c0 + n)])
+
+    dma("S", T.HD[:], T.hd[:], 2.2, [], [W("HD")])
+    for a in range(4):
+        for h in range(2):
+            r0 = 32 * a + 16 * h
+            for e, n, d in (("S", "ZL", 0), ("Y", "ZR", 16)):
+                dma(e, T[n][r0:r0 + 16], T.comp[32 * a + d:32 * a + d + 16, 512 * h:512 * h + 512], 5.0, [], [(n, r0, r0 + 1)])
+    for h in (1, 0):
+        dma("Y", T.NB0[:, HALF * h:HALF * h + HALF], T.lim[:, HALF * h:HALF * h + HALF], 8.0, [], [("NB0", HALF * h, HALF * h + HALF)])
+
+    def load_tiles(t, eng, soft=()):
+        for j in range(5):
+            dma(eng, T["FVT%d" % t][:, 256 * j:256 * j + 256], T.feat[:, 1024 + 256 * t:1280 + 256 * t],
+                4.0, [], [("FVT%d" % t, 256 * j, 256 * j + 256)], soft)
+    load_tiles(0, "S")
+    dma("S", T.FE[:], T.feat[:], 12.0, [], [W("FE")])
+
+    gps(lambda q: q.iota(T.PI[:, 0:1], [[1, 1]], 0, 1), 2, [W("PI")])
+    for n, pat, base, c in (("RI", [[1, 160]], 0, 320), ("RG", [[16, 8], [0, 16]], 0, 256),
+                            ("TW", [[-4096, 16], [0, 16]], 15 * 4096, 512), ("DUP", [[16, 16]], H, 32)):
+        gps(lambda q, n=n, pat=pat, base=base: q.iota(T[n][:], pat, base, 0, allow_small_or_imprecise_dtypes=True), c, [W(n)])
+    ts(T.PM[:, 0:1], T.PI[:, 0:1], 15, A.bitwise_and, 1, [W("PI")], [W("PM")])
+    ts(T.PG[:, 0:1], T.PI[:, 0:1], 112, A.bitwise_and, 1, [W("PI")], [W("PG")])
+    for c, s, d in ((0, "PI", 0), (1, "PM", 0), (2, "PG", 0), (3, "PI", 16), (4, "PG", 15)):
+        ts(T.PF[:, c:c + 1], T[s][:, 0:1], d, A.add, 1, [W(s)], [("PF", c, c + 1)])
+    fill(T.PF[:, 5:6], float(OFF // 32 + 16), 1, ("PF", 5, 6))
+    fill(T.PF[:, 6:7], -0.5, 1, ("PF", 6, 7))
+    SQB, HLF = ("PF", 5, 6), ("PF", 6, 7)
+
+    def eqc(name, n, col, val, src="RI"):
+        ts(T[name][:, 0:n], T[src][:, 0:n], T.PF[:, col:col + 1], A.is_equal, n, [W(src), ("PF", col, col + 1)], [W(name)], val, A.mult)
+    eqc("MB", 160, 3, 1.0)
+    eqc("MK", 16, 1, 1.0)
+    for y in range(16):
+        act(T.MIP[:, 160 * y:160 * y + 160], T.MB[:], F.Copy, 160, [W("MB"), W("MK")], [("MIP", 160 * y, 160 * y + 160)],
+            scale=T.MK[:, y:y + 1], soft=[lastd["S"]])
+    for n, v in (("E1", 1.0), ("ES1", 65536.0), ("E05", 0.5), ("EX", 0.0625), ("ES5", 32768.0), ("ESN", -32768.0)):
+        eqc(n, 144, 4, v)
+    for n, v in (("ID", 1.0), ("IDN", -1.0), ("IDK", float(1 << 28))):
+        eqc(n, 128, 0, v)
+    eqc("BMW", 128, 2, 1.0, "RG")
+    ts(T.DUP[:], T.DUP[:], T.PF[:, 1:2], A.add, 16, [W("DUP"), ("PF", 1, 2)], [W("DUP")])
+    for y in range(16):
+        act(T.BI[:, 128 * y:128 * y + 128], T.BMW[:], F.Copy, 128, [W("BMW"), W("MK")], [("BI", 128 * y, 128 * y + 128)],
+            scale=T.MK[:, y:y + 1], soft=[lastd["S"]])
+        ts(T.TRI[:, y, :], T.RI[:, 0:16], T.PF[:, 1:2], A.is_gt, 16, [W("RI"), ("PF", 1, 2)], [("TRI", 16 * y, 16 * y + 16)])
+    fill(T.ZERO[:], 0.0, 128, W("ZERO"))
+    fill(T.ONES[:], 1.0, 64, W("ONES"))
+    fill(T.KV[:, 0:4], float(BV), 4, ("KV", 0, 4))
+    fill(T.KW[:, 0:4], float(BS), 4, ("KW", 0, 4))
+    for t in range(RT - 1):
+        fill(T["OUTV%d" % t][:, 256:264], 0.0, 4, ("OUTV%d" % t, 256, 264))
+
+    def spread(out, src, c, w):
+        lst = []
+        for i in range(16):
+            for d in (0, 1):
+                lst.append((out(i), T.MIP[:, 161 * i + 16 - d - i + i * 0:161 * i + 144 - d - i], T[src][:, c + d * w:c + d * w + w], d == 0, d == 1, w))
+        return lst
+
+    ts(T.HDI[:, 0:64], T.HD[:], 4080, A.bitwise_and, 64, [W("HD")], [("HDI", 0, 64)])
+    ts(T.HDI[:, 64:128], T.HD[:], 15, A.bitwise_and, 64, [W("HD")], [("HDI", 64, 128)])
+    cp(T.HDB[:], T.HDI[:], 128, [W("HDI")], [W("HDB")])
+
+    def sel(i, d):
+        return T.MIP[:, 160 * i + 16 + i - d:160 * i + 144 + i - d]
+    for b in range(2):
+        bank = "B%d" % b
+        lst = []
+        for y in range(8):
+            o = T[bank][:, 64 * y:64 * y + 64]
+            for d in (0, 1):
+                lst.append((o, sel(8 * b + y, d), T.HDB[:, 64 * d:64 * d + 64], d == 0, d == 1, 64))
+        mms(lst, [W("MIP"), W("HDB")], [(bank, 0, 512)])
+        act(T.HT[:, 512 * b:512 * b + 512], T[bank][:], F.Copy, 512, [(bank, 0, 512)], [("HT", 512 * b, 512 * b + 512)])
+
+    def lists(tp):
+        b0 = 16 * tp
+        zr = ("Z", 32 * b0, 32 * b0 + 512)
+        cp(T.Z[:, b0:b0 + 16, 0:16], T.ZL[:, b0:b0 + 16, :], 256, [W("ZL")], [zr])
+        cp(T.Z[:, b0:b0 + 16, 16:32], T.ZR[:, b0:b0 + 16, :], 256, [W("ZR")], [zr])
+        for b in range(b0, b0 + 16):
+            vec(lambda q, b=b: q.transpose(T.ZT[:, :, b], T.Z[:, b, :]), 32, [zr], [("ZT", 512 * tp, 512 * tp + 512)])
+
+    def permute(t):
+        tp, h = t % 2, t // 2
+        cp(T.LT[:, 256 * t:256 * t + 256], T.ZT[:, 16 * h:16 * h + 16, 16 * tp:16 * tp + 16], 256,
+           [("ZT", 512 * tp, 512 * tp + 512)], [("LT", 256 * t, 256 * t + 256)])
+
+    cores = T.cores
+
+    def rel(src, dst):
+        return (src - dst) % NR
+
+    def addr(dst):
+        return topo.addr(cores[dst])[0:2]
+    onchip = [r for r in range(NR) if r != rank and topo.chip(cores[r]) == topo.chip(core)][0]
+    far = [r for r in range(NR) if topo.chip(cores[r]) != topo.chip(core)]
+    cross = topo.engines(core, cores[far[0]])
+    local = [e for e in topo.engines(core, cores[onchip]) if e not in cross]
+    bulk = []
+
+    def emask(es):
+        return sum(1 << e for e in es)
+
+    def send(src, h, dst, es):
+        s = "ls%d" % nxt("ls", 99)
+        rid, pid = addr(dst)
+        buf = "NB%d" % rel(src, rank)
+        out = T["NB%d" % rel(src, dst)][:, HALF * h:HALF * h + HALF]
+        in_ = T[buf][:, HALF * h:HALF * h + HALF]
+        rs = T.sem["n%d_%d" % (rel(src, dst), h)]
+        bulk.append(add(gr, "G", lambda q: q.remote_dma(out, in_, rs, T.sem[s], pid, rid, emask(es)), 0.8,
+                        [(buf, HALF * h, HALF * h + HALF)], [], "s", s, len(es), 6.0, soft=bulk[-1:]))
+
+    def recv(src, h, est, n):
+        a = rel(src, rank)
+        add(gr, "R", None, 0.0, [], [("NB%d" % a, HALF * h, HALF * h + HALF)], "r", "n%d_%d" % (a, h), n, est=est)
+
+    first = rank if (rank - 1) % NR in far else onchip
+    second = onchip if first == rank else rank
+    o_first = [r for r in far if (r - 1) % NR not in far][0]
+    o_second = [r for r in far if r != o_first][0]
+    gate, mygate = (first - 1) % NR, (o_first - 1) % NR
+    recv(onchip, 1, 10.0, len(local))
+    recv(onchip, 0, 14.0, len(local))
+    late = 0.0 if rank == mygate else 6.0
+    nin = len(cross) if rank == mygate else len(local) + len(cross)
+    for src, e in ((o_first, 20.0), (o_second, 30.0)):
+        for h in range(2):
+            recv(src, h, e + late, nin)
+    send(rank, 1, onchip, local)
+    if rank == first:
+        send(rank, 0, gate, cross)
+        send(rank, 0, onchip, local)
+        send(second, 1, gate, cross)
+    else:
+        send(rank, 0, onchip, local)
+        send(first, 1, gate, cross)
+        send(rank, 0, gate, cross)
+    if rank == mygate:
+        for src in (o_first, o_second):
+            for h in range(2):
+                send(src, h, onchip, local + cross)
+
+    def shares(t, vch=(), soft=()):
+        key, fv, n = "KEY%d" % (t % 2), "FVT%d" % t, 1024 + 256 * t
+        mms([(T[key][:, 0:256], T.ID[:], T.ZERO[:], True, False, 256)], [W("ID"), W("ZERO")], [(key, 0, 256)])
+        for ch in range(4):
+            c = 256 * t + 64 * ch
+            if ch in vch:
+                x = "XH%d" % (ch // 2)
+                tt(T[x][:], T.FE[:, 0:n].indirect(T.LT[:, c:c + 64]), T[fv][:, 0:1024], A.min, 1024 * GC,
+                   [W("FE"), ("LT", c, c + 64), W(fv)], [W(x)])
+                extract(key, 64 * ch, [("ES1", x)], False, False)
+            else:
+                x, s = "GH%d" % (ch % 2), "SH%d" % (ch % 2)
+                for hh in range(2):
+                    sl = slice(512 * hh, 512 * hh + 512)
+                    o = c + 32 * hh
+                    xr, sr = (x, sl.start, sl.stop), (s, sl.start, sl.stop)
+                    act(T[x][:, sl], T.FE[:, 0:n].indirect(T.LT[:, o:o + 32]), F.Copy, 512 * GC, [W("FE"), ("LT", o, o + 32)], [xr], soft=soft)
+                    mms([(T.B5[:], T.ID[:], T[fv][:, sl], True, False, 512), (T.B5[:], T.IDN[:], T[x][:, sl], False, True, 512)],
+                        [W("ID"), W("IDN"), W(fv), xr], [W("B5")])
+                    act(T[s][:, sl], T.B5[:], F.Abs, 512, [W("B5")], [sr])
+                extract(key, 64 * ch, [("ES5", x), ("ESN", s)] + ([("ES5", fv)] if vch else []), False, False)
+
+    def square(sl):
+        r = sl.start, sl.stop
+        act(T.SQ[:, sl], T.C32[:, sl], F.Square, r[1] - r[0], [("C32",) + r, SQB], [("SQ",) + r], bias=T.PF[:, 5:6], scale=1.0 / 32)
+
+    def gather_headings(t):
+        n = 1024 + 256 * t
+        for k0, kn, eng in CHUNKS:
+            c, w = 256 * t + 16 * k0, 16 * kn
+            src = T.HT[:, 0:n].indirect(T.LT[:, c:c + w])
+            rd = [("HT", 0, n), ("LT", c, c + w)]
+            if eng == "V":
+                x = "XV%d" % nxt("x", 4)
+                cp(T[x][:, 0:16 * w], src, 16 * w * GC, rd, [W(x)])
+            else:
+                x = "GS%d" % nxt("s", 4)
+                act(T[x][:, 0:16 * w], src, F.Copy, 16 * w * GC, rd, [W(x)])
+            bank = "B%d" % nxt("b", 3)
+            extract(bank, 0, [("E1", x)], True, True, w)
+            sl = slice(16 * k0, 16 * k0 + w)
+            cp(T.CL0[:, sl], T[bank][:, 0:w], w, [(bank, 0, w)], [("CL0", sl.start, sl.stop)])
+            ts(T.C32[:, sl], T[bank][:, 0:w], 32.0, A.mult, w, [(bank, 0, w)], [("C32", sl.start, sl.stop)], float(-OFF), A.add)
+            square(sl)
+
+    def visits(t):
+        fv = "FVT%d" % t
+        for a in range(NR):
+            nb, cl, cln = "NB%d" % a, "CL%d" % (a % 2), "CL%d" % (1 - a % 2)
+            if a > 0 and t > 0:
+                apply_update(t - 1, a)
+            for k0, kn, eng in CHUNKS:
+                w = 16 * kn
+                e16 = 16 * w
+                sl = slice(16 * k0, 16 * k0 + w)
+                bank = "B%d" % nxt("b", 3)
+                src = T[nb][:, 0:H].indirect(T[cl][:, sl])
+
+                def C(n):
+                    return (n, sl.start, sl.stop)
+                if eng == "V":
+                    x, kb = "XV%d" % nxt("x", 4), "KV"
+                    tt(T[x][:, 0:e16], src, T[fv][:, 0:e16], A.is_lt, e16 * GC, [(nb, 0, H), C(cl), W(fv)], [W(x)])
+                    extract(bank, 0, [("E1", x)], True, True, w)
+                else:
+                    j = nxt("s", 4)
+                    x, s, kb = "GS%d" % j, "SS%d" % j, "KW"
+                    act(T[x][:, 0:e16], src, F.Copy, e16 * GC, [(nb, 0, H), C(cl)], [W(x)])
+                    for hh in range(2):
+                        u = slice(512 * hh, min(e16, 512 * hh + 512))
+                        m = u.stop - u.start
+                        db = "B%d" % (3 + hh)
+                        mms([(T[db][:, 0:m], T.ID[:], T[fv][:, u], True, False, m), (T[db][:, 0:m], T.IDN[:], T[x][:, u], False, True, m)],
+                            [W("ID"), W("IDN"), W(fv), W(x)], [W(db)])
+                        last = act(T[s][:, u], T[db][:, 0:m], F.Sign, m, [W(db), HLF], [(s, u.start, u.stop)], bias=T.PF[:, 6:7])
+                    extract(bank, 0, [("E05", s)], True, True, w)
+                P, pr, kc = T[bank][:, 0:w], (bank, 0, w), 4 * t + a
+                ts(P, P, float(SLOPE), A.mult, w, [pr, (kb, kc, kc + 1)], [pr], T[kb][:, kc:kc + 1], A.add)
+                tt(P, P, T.SQ[:, sl], A.add, w, [pr, C("SQ")], [pr])
+                tt(T.TI[:, sl], P, T.C32[:, sl], A.max, w, [pr, C("C32")], [C("TI")])
+                ts(T.CI[:, sl], T.TI[:, sl], 5, A.arith_shift_right, w, [C("TI")], [C("CI")], 4095, A.bitwise_and)
+                if a < NR - 1:
+                    cp(T[cln][:, sl], T.CI[:, sl], w, [C("CI")], [C(cln)])
+                    ts(T.C32[:, sl], T.CI[:, sl], 32.0, A.mult, w, [C("CI")], [C("C32")], float(-OFF), A.add)
+                    square(sl)
+                else:
+                    cp(T.CW[:, sl], T.CI[:, sl], w, [C("CI")], [C("CW")])
+        return last
+
+    def election(t):
+        key = "KEY%d" % (t % 2)
+        C2 = ("B2", 0, 256)
+        act(T.B2[:, 0:256], T.CW[:, 0:256], F.Copy, 256, [("CW", 0, 256)], [C2])
+        act(T.CW[:, 256:384], T.CW[:, 0:128], F.Copy, 128, [("CW", 0, 128)], [("CW", 256, 384)])
+
+        def K(a, b):
+            return T[key][:, a:b]
+        for d in range(1, 9):
+            n, s, e = (256 if d < 8 else 128), 16 * d, ("EQ", 256 * d, 256 * d + 256)
+            tt(T.EQ[:, d, 0:n], T.B2[:, 0:n], T.CW[:, s:s + n], A.is_equal, n, [C2, ("CW", s, s + n)], [e])
+            lst = [(K(0, n), T.IDK[:], T.EQ[:, d, 0:n], False, False, n),
+                   (K(s, 256), T.IDK[:], T.EQ[:, d, 0:256 - s], False, d == 8, 256 - s)]
+            if d < 8:
+                lst.append((K(0, s), T.IDK[:], T.EQ[:, d, 256 - s:256], False, False, s))
+            mms(lst, [e, W("IDK")], [(key, 0, 256)])
+        kr = (key, 0, 256)
+        tt(T.KK[:, 256:512], T.TW[:], K(0, 256), A.subtract, 256, [W("TW"), kr], [("KK", 256, 512)])
+        tt(T.KK[:, 0:256], K(0, 256), T.TW[:], A.add, 256, [W("TW"), kr], [("KK", 0, 256)])
+
+        def tree(src, w, out, oc):
+            n, s, so = 128, src, 256 * w
+            for m in ("M1", "M2", "M3", None):
+                dst, do = (out, oc) if m is None else (m, n * w)
+                tt(T[dst][:, do:do + n], T[s][:, so:so + n], T[s][:, so + n:so + 2 * n], A.max, 2 * n, [(s, so, so + 2 * n)], [(dst, do, do + n)])
+                n, s, so = n // 2, dst, do
+        tree("KK", 1, "B4", 0)
+        tree("KK", 0, "B3", 0)
+        n = 16
+        while n < 256:
+            for b in ("B4", "B3"):
+                cp(T[b][:, n:2 * n], T[b][:, 0:n], n, [(b, 0, n)], [(b, n, 2 * n)])
+            n *= 2
+        for b, w in (("B4", 1), ("B3", 0)):
+            c = slice(256 * w, 256 * w + 256)
+            q = ("DD", c.start, c.stop)
+            tt(T.DD[:, c], T.KK[:, c], T[b][:, 0:256], A.subtract, 256, [("KK", c.start, c.stop), (b, 0, 256)], [q])
+            tt(T.DD[:, c], T.DD[:, c], T.B2[:, 0:256], A.add, 256, [q, C2], [q])
+            tree("DD", w, "WLI", 16 * w)
+        for w in (1, 0):
+            rd, o = ("WLI", 16 * w, 16 * w + 16), 32 * w
+            for d, m in ((0, 4080), (16, 15)):
+                ts(T.SPI[:, o + d:o + d + 16], T.WLI[:, 16 * w:16 * w + 16], m, A.bitwise_and, 16, [rd], [("SPI", o + d, o + d + 16)])
+            cp(T.SPB[:, o:o + 32], T.SPI[:, o:o + 32], 32, [("SPI", o, o + 32)], [("SPB", o, o + 32)])
+        for n in ("LF", "LU"):
+            cp(T[n][:], T.WLI[:, 16:32], 16, [("WLI", 16, 32)], [W(n)])
+
+    def headings_out(t):
+        lst = []
+        for i in range(16):
+            for d in (0, 1):
+                lst.append((T.B0[:, i:256:16], sel(i, d), T.SPB[:, 16 * d:16 * d + 16], d == 0, d == 1, 16))
+        mms(lst, [("SPB", 0, 32), W("MIP")], [("B0", 0, 256)])
+        c = 1024 + 256 * t
+        act(T.HT[:, c:c + 256], T.B0[:, 0:256], F.Copy, 256, [("B0", 0, 256)], [("HT", c, c + 256)])
+
+    def write_yh(t):
+        c, y = 1024 + 256 * t, ("YH8", 256 * t, 256 * t + 256)
+        mms([(T.B5[0:8, 0:256], T.BMW[:, 0:128:16], T.HT[:, c:c + 256], True, True, 256)], [W("BMW"), ("HT", c, c + 256)], [("B5", 0, 256)])
+        act(T.YH8[:, 256 * t:256 * t + 256], T.B5[0:8, 0:256], F.Copy, 256, [("B5", 0, 256)], [y])
+        dma("Y", T.yh[:, 256 * t:256 * t + 256], T.YH8[:, 256 * t:256 * t + 256], 2.5, [y], [])
+
+    def notes(t):
+        fv, ov, ol = "FVT%d" % t, "OUTV%d" % t, "OUTL%d" % t
+        b1, b3, b4 = ("B1", 0, 256), ("B3", 0, 256), ("B4", 0, 256)
+        act(T.OLD[:], T.NB0[:, 0:H].indirect(T.LU[:, 0:16]), F.Copy, 256 * GC, [("NB0", 0, H), W("LU")], [W("OLD")])
+        mms([(T.B3[:, 0:256], T.ID[:], T[fv][:, 0:256], True, False, 256), (T.B3[:, 0:256], T.IDN[:], T.OLD[:], False, True, 256)],
+            [W("ID"), W("IDN"), W(fv), W("OLD")], [b3])
+        ts(T.DC[:], T.B3[:, 0:256], 32.0, A.min, 256, [b3], [W("DC")], -32.0, A.max)
+        mms([(T.B4[:, 0:256], T.ID[:], T.OLD[:], True, False, 256), (T.B4[:, 0:256], T.ID[:], T.DC[:], False, True, 256)],
+            [W("ID"), W("OLD"), W("DC")], [b4])
+        act(T[ov][:, 0:256], T.B4[:, 0:256], F.Copy, 256, [b4], [(ov, 0, 256)])
+        lst = []
+        for i in range(16):
+            for d in (0, 1):
+                lst.append((T.B1[:, i:256:16], T.BI[:, 128 * i:128 * i + 128], T.SPB[:, 32 + 16 * d:48 + 16 * d], d == 0, d == 1, 16))
+        mms(lst, [("SPB", 32, 64), W("BI")], [b1])
+        cp(T.LB[:], T.B1[:, 0:256], 256, [b1], [W("LB")])
+        for lo in (0, 8):
+            er = ("EQT", 256 * lo, 256 * lo + 2048)
+            for mb in range(lo, lo + 8):
+                n = 256 - 16 * mb
+                ts(T.EQT[:, mb, 0:n], T.LB[:, 16 * mb:256], T.LF[:, mb:mb + 1], A.is_equal, n * 0.5, [W("LB"), W("LF")], [("EQT", 256 * mb, 256 * mb + 256)])
+            tt(T.EQT[:, lo:lo + 8, 0:16], T.EQT[:, lo:lo + 8, 0:16], T.TRI[:, lo:lo + 8, :], A.mult, 256, [er, W("TRI")], [er])
+            mms([(T.B1[:, 16 * mb:256], T.BMW[:], T.EQT[:, mb, 0:256 - 16 * mb], mb == 0, mb == 15, 256 - 16 * mb) for mb in range(lo, lo + 8)],
+                [W("BMW"), er], [b1])
+        ts(T.FL[:], T.B1[:, 0:256], 0.5, A.is_gt, 256, [b1], [W("FL")])
+        mms([(T.B1[:, 256:272], T.EX[:, 15 - i:143 - i], T.FL[:, i:256:16], i == 0, i == 15, 16) for i in range(16)],
+            [W("EX"), W("FL")], [("B1", 256, 272)])
+        tt(T.DL[:], T.DUP[:], T.LF[:], A.subtract, 32, [W("DUP"), W("LF")], [W("DL")])
+        tt(T.OF[:], T.B1[:, 256:272], T.DL[:], A.mult, 32, [("B1", 256, 272), W("DL")], [W("OF")])
+        tt(T.OF[:], T.OF[:], T.LF[:], A.add, 32, [W("OF"), W("LF")], [W("OF")])
+        cp(T[ol][:], T.OF[:], 16, [W("OF")], [W(ol)])
+        scatter("NB0", ov, ol)
+
+    def scatter(nb, ov, ol):
+        vec(lambda q: q.tensor_copy(out=T[nb][:, 0:H + DUMMY].indirect(T[ol][:, 0:16]), in_=T[ov][:, 0:256]), 256 * 3,
+            [(ov, 0, 256), W(ol)], [(nb, 0, H + DUMMY)])
+
+    def bias(t, a, src):
+        c = 4 * (t + 1) + a
+        for kb, v in (("KV", BV), ("KW", BS)):
+            ts(T[kb][:, c:c + 1], T[src][:, 256:257], 32.0, A.mult, 1, [(src, 256, 257)], [(kb, c, c + 1)], float(v), A.add)
+
+    def kappa(t):
+        ov = "OUTV%d" % t
+        mms([(T.B0[:, 0:32], T.ONES[:], T.SPB[:, 0:32], True, True, 32)], [W("ONES"), ("SPB", 0, 32)], [("B0", 0, 32)])
+        act(T.JUNK[:], T.B0[:, 0:32], F.Copy, 32, [("B0", 0, 32)], [W("KS1"), W("JUNK")], accum=T.KS1[:, 0:1])
+        cp(T.KI[:, 0:1], T.KS1[:, 0:1], 1, [W("KS1")], [W("KI")])
+        ts(T.KJ[:, 0:1], T.KI[:, 0:1], 255, A.bitwise_and, 1, [W("KI")], [W("KJ")])
+        cp(T[ov][:, 256:257], T.KJ[:, 0:1], 1, [W("KJ")], [(ov, 256, 257)])
+        bias(t, 0, ov)
+
+    sent = {}
+
+    def send_update(t):
+        dsts = [(rank - a) % NR for a in range(1, NR)]
+        ids = [DstId(rid=addr(x)[0], pnc=addr(x)[1]) for x in dsts]
+        for nm, inn, sm in (("OUTL%d" % t, "INL%d_%d", "il%d_%d"), ("OUTV%d" % t, "INV%d_%d", "iv%d_%d")):
+            def f(q, nm=nm, inn=inn, sm=sm):
+                tr = RemoteDMATransfer(dst_ids=ids, dma_engine_mask=emask(cross), remote_sem=T.sem[sm % (rank, t)], srcs=[T[nm][:]],
+                                       dsts=[T[inn % (rel(rank, x), t)][:] for x in dsts])
+                return q.remote_dma_fused([tr], local_sem=T.sem.lsend)
+            num["lsend"] += len(cross)
+            bulk.append(add(gr, "G", f, 1.2, [W(nm)], [], "s", "lsend", num["lsend"], soft=bulk[-1:]))
+        sent[t] = bulk[-1]
+
+    def apply_update(t, a):
+        iv, il = "INV%d_%d" % (a, t), "INL%d_%d" % (a, t)
+        src = (rank + a) % NR
+        for nm, sm in ((il, "il%d_%d"), (iv, "iv%d_%d")):
+            add(gr, "R", None, 0.0, [], [W(nm)], "r", sm % (src, t), len(cross), 3.5, soft=[sent[t]])
+        bias(t, a, iv)
+        scatter("NB%d" % a, iv, il)
+
+    lists(0)
+    permute(0)
+    gather_headings(0)
+    shares(0, SHARE0)
+    first_v = len(gr["nodes"]) - 1
+    lists(1)
+    for t in range(1, RT):
+        permute(t)
+        load_tiles(t, "Y", [first_v])
+    for t in range(RT):
+        last = visits(t)
+        if t + 1 < RT:
+            shares(t + 1, (), [last])
+        election(t)
+        headings_out(t)
+        notes(t)
+        if t + 1 < RT:
+            gather_headings(t + 1)
+            kappa(t)
+            send_update(t)
+        write_yh(t)
+    for j, e in ((0, "S"), (1, "Y")):
+        dma(e, T.yl[:, HALF * j:HALF * j + HALF], T.NB0[:, HALF * j:HALF * j + HALF], 5.0, [("NB0", HALF * j, HALF * j + HALF)], [])
+    return gr
+
+
+def rank_program(g, core, T, topo):
+    if T.rank_of(core) is None:
+        return
+    gr = build(core, T, topo)
+    emit_all(gr, schedule(gr), g, T)

@@ -8,10 +8,10 @@ SLOPE = 613 * 32 + MOD * KS
 OFF = MOD * 512
 BV = -256 - MOD * (9 * KS + 1) - OFF
 BS = BV + 8 * SLOPE
-CHUNKS = ((0, 5, "V"), (5, 4, "S"), (9, 4, "V"), (13, 3, "S"))
-SHARE0 = (0, 2)
+CHUNKS = ((0, 4, "V", "V"), (4, 4, "S", "S"), (8, 5, "V", "S"), (13, 3, "S", "S"))
+SHARE_V = (0, 2)
+PIECE = 512
 CYC, GC, PEC = 0.83e-3 * 1.25, 1.56, 0.68e-3
-LOOK, LSAME, LCROSS = 0.3, 0.0, 0.0
 
 SCRATCH = {}
 SEMAPHORES = ["cv", "cs", "cp", "cg", "lsend"] + ["d%d" % j for j in range(52)] + ["ls%d" % j for j in range(10)]
@@ -25,7 +25,7 @@ def _buf(names, cols, dtype, where="sbuf", rows=128):
 B16, F32, I32, U16 = "bfloat16", "float32", "int32", "uint16"
 _buf("NB0 NB1 NB2 NB3", H + DUMMY, B16)
 _buf("FE HT", 2048, B16)
-_buf("FVT0 FVT1 FVT2 FVT3 XV0 XV1 XV2 XV3", 1280, B16)
+_buf("FVT0 FVT1 FVT2 FVT3 XV0 XV1 XV2 XV3 GS0 GS1 GS2 GS3", 1280, B16)
 _buf("OUTV0 OUTV1 OUTV2 OUTV3", 264, B16)
 _buf("OUTL0 OUTL1 OUTL2 OUTL3 LU", 16, U16)
 for _t in range(RT - 1):
@@ -51,10 +51,11 @@ _buf("MB", 160, B16)
 _buf("MIP", 16 * 160, B16)
 _buf("BI", 16 * 128, B16)
 _buf("E1 E05 ES1 ES5 ESN EX", 144, B16)
-_buf("ZERO FL OLD DC", 256, B16)
+_buf("FL OLD DC", 256, B16)
+_buf("SW SL", 1024, F32)
 _buf("TW C32 SQ M1", 256, F32)
 _buf("TRI", [16, 16], B16)
-_buf("GS0 GS1 GS2 GS3 SS0 SS1 SS2 SS3 XH0 XH1 GH0 GH1 SH0 SH1", 1024, B16)
+_buf("SS0 SS1 SS2 SS3 XH0 XH1 GH0 GH1 SH0 SH1", 1024, B16)
 _buf("CL0 CL1 LB", 256, U16)
 _buf("TI CI", 256, I32)
 _buf("CW", 384, F32)
@@ -128,22 +129,14 @@ def schedule(gr):
                     best = (s, e)
         s, e = best
         i = max((k for k in ready[e] if at[k] <= s), key=lambda k: (rank[k], -k))
-        if nodes[i]["cost"] > 0.4:
-            for k in sorted(ready[e]):
-                if at[k] <= s + LOOK * nodes[i]["cost"] and rank[k] > rank[i]:
-                    i = k
         n = nodes[i]
-        s = max(free[e], at[i])
         ready[e].discard(i)
         if e != "R":
             free[e] = s + n["cost"]
         order.append(i)
         for k in succ[i]:
             left[k] -= 1
-            f = s + n["cost"]
-            if i in nodes[k]["deps"]:
-                f += n["lat"] + (LSAME if nodes[k]["eng"] == e else LCROSS)
-            at[k] = max(at[k], f)
+            at[k] = max(at[k], s + n["cost"] + (n["lat"] if i in nodes[k]["deps"] else 0.0))
             if left[k] == 0:
                 ready[nodes[k]["eng"]].add(k)
     return order
@@ -205,7 +198,7 @@ def build(core, T, topo):
         return (n, 0, 1 << 20)
 
     def vec(fn, cyc, reads, writes):
-        return add(gr, "V", fn, max(64, cyc) * CYC + 0.02, reads, writes)
+        return add(gr, "V", fn, max(64, cyc) * CYC + 0.04, reads, writes)
 
     def gps(fn, cyc, writes):
         return add(gr, "G", fn, cyc * CYC + 0.15, [], writes)
@@ -234,38 +227,42 @@ def build(core, T, topo):
             if accum is not None:
                 return q.activation(out=out, in_=in_, func=func, bias=bias, scale=scale, accum_out=accum)
             return q.activation(out=out, in_=in_, func=func, bias=bias, scale=scale)
-        return add(gr, "S", f, max(64, cyc) * CYC + 0.04, reads, writes, soft=soft)
+        return add(gr, "S", f, max(64, cyc) * CYC + 0.1, reads, writes, soft=soft)
 
-    def mms(lst, reads, writes):
+    def mms(lst, reads, writes, soft=()):
         def f(q):
             for (o, l, r, st, sp, _) in lst:
                 ins = q.matmul(o, l, r, st, sp)
             return ins
-        return add(gr, "P", f, sum(max(64, x[5]) for x in lst) * PEC + 0.03, reads, writes)
+        return add(gr, "P", f, sum(max(64, x[5]) for x in lst) * PEC + 0.03, reads, writes, soft=soft)
 
-    def extract(bank, c0, parts, start, stop, n=64):
-        lst = []
-        for en, x in parts:
-            for i in range(16):
-                lst.append((T[bank][:, c0:c0 + n], T[en][:, 15 - i:143 - i], T[x][:, i:16 * n:16],
-                            start and not lst, stop and len(lst) == 16 * len(parts) - 1, n))
-        return mms(lst, [(x, 0, 16 * n) for _, x in parts] + [W(en) for en, _ in parts], [(bank, c0, c0 + n)])
+    def extract(bank, c0, en, x, start, stop, n=64, reg=None):
+        return mms([(T[bank][:, c0:c0 + n], T[en][:, 15 - i:143 - i], T[x][:, i:16 * n:16], start and i == 0, stop and i == 15, n)
+                    for i in range(16)], [(x, 0, 16 * n), W(en)], [reg or (bank, c0, c0 + n)])
+
+    def pieces(n, c):
+        return [(slice(j, min(n, j + PIECE)), slice(c + j // 16, c + min(n, j + PIECE) // 16)) for j in range(0, n, PIECE)]
+
+    def subtract(bank, fv, u, x):
+        m = u.stop - u.start
+        mms([(T[bank][:, 0:m], T.ID[:], T[fv][:, u], True, False, m)], [W("ID"), W(fv)], [W(bank)])
+        mms([(T[bank][:, 0:m], T.IDN[:], T[x][:, u], False, True, m)], [W("IDN"), (x, u.start, u.stop)], [W(bank)])
 
     dma("S", T.HD[:], T.hd[:], 2.2, [], [W("HD")])
     for a in range(4):
         for h in range(2):
             r0 = 32 * a + 16 * h
             for e, n, d in (("S", "ZL", 0), ("Y", "ZR", 16)):
-                dma(e, T[n][r0:r0 + 16], T.comp[32 * a + d:32 * a + d + 16, 512 * h:512 * h + 512], 5.0, [], [(n, r0, r0 + 1)])
-    for h in (1, 0):
-        dma("Y", T.NB0[:, HALF * h:HALF * h + HALF], T.lim[:, HALF * h:HALF * h + HALF], 8.0, [], [("NB0", HALF * h, HALF * h + HALF)])
+                dma(e, T[n][r0:r0 + 16], T.comp[32 * a + d:32 * a + d + 16, 512 * h:512 * h + 512], 6.5, [], [(n, r0, r0 + 1)])
+    for h in (0, 1):
+        dma("Y", T.NB0[:, HALF * h:HALF * h + HALF], T.lim[:, HALF * h:HALF * h + HALF], 11.0, [], [("NB0", HALF * h, HALF * h + HALF)])
+    dma("S", T.FVT0[:, 0:256], T.feat[:, 1024:1280], 13.0, [], [("FVT0", 0, 256)])
+    dma("S", T.FE[:], T.feat[:], 16.0, [], [W("FE")])
 
-    def load_tiles(t, eng, soft=()):
+    def load_tiles(t, soft):
         for j in range(5):
-            dma(eng, T["FVT%d" % t][:, 256 * j:256 * j + 256], T.feat[:, 1024 + 256 * t:1280 + 256 * t],
+            dma("Y", T["FVT%d" % t][:, 256 * j:256 * j + 256], T.feat[:, 1024 + 256 * t:1280 + 256 * t],
                 4.0, [], [("FVT%d" % t, 256 * j, 256 * j + 256)], soft)
-    load_tiles(0, "S")
-    dma("S", T.FE[:], T.feat[:], 12.0, [], [W("FE")])
 
     gps(lambda q: q.iota(T.PI[:, 0:1], [[1, 1]], 0, 1), 2, [W("PI")])
     for n, pat, base, c in (("RI", [[1, 160]], 0, 320), ("RG", [[16, 8], [0, 16]], 0, 256),
@@ -275,9 +272,9 @@ def build(core, T, topo):
     ts(T.PG[:, 0:1], T.PI[:, 0:1], 112, A.bitwise_and, 1, [W("PI")], [W("PG")])
     for c, s, d in ((0, "PI", 0), (1, "PM", 0), (2, "PG", 0), (3, "PI", 16), (4, "PG", 15)):
         ts(T.PF[:, c:c + 1], T[s][:, 0:1], d, A.add, 1, [W(s)], [("PF", c, c + 1)])
-    fill(T.PF[:, 5:6], float(OFF // 32 + 16), 1, ("PF", 5, 6))
-    fill(T.PF[:, 6:7], -0.5, 1, ("PF", 6, 7))
-    SQB, HLF = ("PF", 5, 6), ("PF", 6, 7)
+    for c, v in ((5, OFF // 32 + 16), (6, -0.5), (7, -OFF)):
+        fill(T.PF[:, c:c + 1], float(v), 1, ("PF", c, c + 1))
+    SQB, HLF, MOFF = ("PF", 5, 6), ("PF", 6, 7), ("PF", 7, 8)
 
     def eqc(name, n, col, val, src="RI"):
         ts(T[name][:, 0:n], T[src][:, 0:n], T.PF[:, col:col + 1], A.is_equal, n, [W(src), ("PF", col, col + 1)], [W(name)], val, A.mult)
@@ -296,19 +293,13 @@ def build(core, T, topo):
         act(T.BI[:, 128 * y:128 * y + 128], T.BMW[:], F.Copy, 128, [W("BMW"), W("MK")], [("BI", 128 * y, 128 * y + 128)],
             scale=T.MK[:, y:y + 1], soft=[lastd["S"]])
         ts(T.TRI[:, y, :], T.RI[:, 0:16], T.PF[:, 1:2], A.is_gt, 16, [W("RI"), ("PF", 1, 2)], [("TRI", 16 * y, 16 * y + 16)])
-    fill(T.ZERO[:], 0.0, 128, W("ZERO"))
     fill(T.ONES[:], 1.0, 64, W("ONES"))
     fill(T.KV[:, 0:4], float(BV), 4, ("KV", 0, 4))
     fill(T.KW[:, 0:4], float(BS), 4, ("KW", 0, 4))
     for t in range(RT - 1):
         fill(T["OUTV%d" % t][:, 256:264], 0.0, 4, ("OUTV%d" % t, 256, 264))
-
-    def spread(out, src, c, w):
-        lst = []
-        for i in range(16):
-            for d in (0, 1):
-                lst.append((out(i), T.MIP[:, 161 * i + 16 - d - i + i * 0:161 * i + 144 - d - i], T[src][:, c + d * w:c + d * w + w], d == 0, d == 1, w))
-        return lst
+    for c0, c1, w in ((256, 512, 256), (512, 1024, 512), (1024, 1280, 256)):
+        cp(T.FVT0[:, c0:c1], T.FVT0[:, 0:w], w // 2, [("FVT0", 0, w)], [("FVT0", c0, c1)])
 
     ts(T.HDI[:, 0:64], T.HD[:], 4080, A.bitwise_and, 64, [W("HD")], [("HDI", 0, 64)])
     ts(T.HDI[:, 64:128], T.HD[:], 15, A.bitwise_and, 64, [W("HD")], [("HDI", 64, 128)])
@@ -318,12 +309,8 @@ def build(core, T, topo):
         return T.MIP[:, 160 * i + 16 + i - d:160 * i + 144 + i - d]
     for b in range(2):
         bank = "B%d" % b
-        lst = []
-        for y in range(8):
-            o = T[bank][:, 64 * y:64 * y + 64]
-            for d in (0, 1):
-                lst.append((o, sel(8 * b + y, d), T.HDB[:, 64 * d:64 * d + 64], d == 0, d == 1, 64))
-        mms(lst, [W("MIP"), W("HDB")], [(bank, 0, 512)])
+        mms([(T[bank][:, 64 * y:64 * y + 64], sel(8 * b + y, d), T.HDB[:, 64 * d:64 * d + 64], d == 0, d == 1, 64)
+             for y in range(8) for d in (0, 1)], [W("MIP"), W("HDB")], [(bank, 0, 512)])
         act(T.HT[:, 512 * b:512 * b + 512], T[bank][:], F.Copy, 512, [(bank, 0, 512)], [("HT", 512 * b, 512 * b + 512)])
 
     def lists(tp):
@@ -350,6 +337,7 @@ def build(core, T, topo):
     far = [r for r in range(NR) if topo.chip(cores[r]) != topo.chip(core)]
     cross = topo.engines(core, cores[far[0]])
     local = [e for e in topo.engines(core, cores[onchip]) if e not in cross]
+    wide = local + cross
     bulk = []
 
     def emask(es):
@@ -370,52 +358,54 @@ def build(core, T, topo):
         add(gr, "R", None, 0.0, [], [("NB%d" % a, HALF * h, HALF * h + HALF)], "r", "n%d_%d" % (a, h), n, est=est)
 
     first = rank if (rank - 1) % NR in far else onchip
-    second = onchip if first == rank else rank
     o_first = [r for r in far if (r - 1) % NR not in far][0]
     o_second = [r for r in far if r != o_first][0]
     gate, mygate = (first - 1) % NR, (o_first - 1) % NR
-    recv(onchip, 1, 10.0, len(local))
-    recv(onchip, 0, 14.0, len(local))
+    nown = len(wide) if rank == first else len(local)
+    recv(onchip, 1, 10.0, nown)
+    recv(onchip, 0, 14.0, nown)
     late = 0.0 if rank == mygate else 6.0
-    nin = len(cross) if rank == mygate else len(local) + len(cross)
-    for src, e in ((o_first, 20.0), (o_second, 30.0)):
+    nin = len(cross) if rank == mygate else len(wide)
+    for src, e in ((o_first, 24.0), (o_second, 34.0)):
         for h in range(2):
             recv(src, h, e + late, nin)
-    send(rank, 1, onchip, local)
     if rank == first:
-        send(rank, 0, gate, cross)
-        send(rank, 0, onchip, local)
-        send(second, 1, gate, cross)
+        for h in range(2):
+            send(rank, h, gate, cross)
+        for h in range(2):
+            send(rank, h, onchip, local)
     else:
-        send(rank, 0, onchip, local)
-        send(first, 1, gate, cross)
-        send(rank, 0, gate, cross)
+        for h in range(2):
+            send(rank, h, onchip, wide)
+        for h in range(2):
+            send(rank, h, gate, cross)
     if rank == mygate:
         for src in (o_first, o_second):
             for h in range(2):
-                send(src, h, onchip, local + cross)
+                send(src, h, onchip, wide)
 
-    def shares(t, vch=(), soft=()):
-        key, fv, n = "KEY%d" % (t % 2), "FVT%d" % t, 1024 + 256 * t
-        mms([(T[key][:, 0:256], T.ID[:], T.ZERO[:], True, False, 256)], [W("ID"), W("ZERO")], [(key, 0, 256)])
-        for ch in range(4):
+    def shares(t):
+        fv, n, kb = "FVT%d" % t, 1024 + 256 * t, W("KEY1")
+        for ch in sorted(range(4), key=lambda x: x not in SHARE_V):
             c = 256 * t + 64 * ch
-            if ch in vch:
+            if ch in SHARE_V:
                 x = "XH%d" % (ch // 2)
                 tt(T[x][:], T.FE[:, 0:n].indirect(T.LT[:, c:c + 64]), T[fv][:, 0:1024], A.min, 1024 * GC,
                    [W("FE"), ("LT", c, c + 64), W(fv)], [W(x)])
-                extract(key, 64 * ch, [("ES1", x)], False, False)
+                extract("KEY1", 64 * ch, "ES1", x, True, True, reg=kb)
             else:
                 x, s = "GH%d" % (ch % 2), "SH%d" % (ch % 2)
-                for hh in range(2):
-                    sl = slice(512 * hh, 512 * hh + 512)
-                    o = c + 32 * hh
-                    xr, sr = (x, sl.start, sl.stop), (s, sl.start, sl.stop)
-                    act(T[x][:, sl], T.FE[:, 0:n].indirect(T.LT[:, o:o + 32]), F.Copy, 512 * GC, [W("FE"), ("LT", o, o + 32)], [xr], soft=soft)
-                    mms([(T.B5[:], T.ID[:], T[fv][:, sl], True, False, 512), (T.B5[:], T.IDN[:], T[x][:, sl], False, True, 512)],
-                        [W("ID"), W("IDN"), W(fv), xr], [W("B5")])
-                    act(T[s][:, sl], T.B5[:], F.Abs, 512, [W("B5")], [sr])
-                extract(key, 64 * ch, [("ES5", x), ("ESN", s)] + ([("ES5", fv)] if vch else []), False, False)
+                for u, o in pieces(1024, c):
+                    act(T[x][:, u], T.FE[:, 0:n].indirect(T.LT[:, o]), F.Copy, (u.stop - u.start) * GC,
+                        [W("FE"), ("LT", o.start, o.stop)], [(x, u.start, u.stop)])
+                    subtract("B5", fv, u, x)
+                    act(T[s][:, u], T.B5[:], F.Abs, u.stop - u.start, [W("B5")], [(s, u.start, u.stop)])
+                extract("KEY1", 64 * ch, "ES5", fv, True, False, reg=kb)
+                extract("KEY1", 64 * ch, "ES5", x, False, False, reg=kb)
+                extract("KEY1", 64 * ch, "ESN", s, False, True, reg=kb)
+        c = slice(256 * t, 256 * t + 256)
+        tt(T.SW[:, c], T.KEY1[:, 0:256], T.TW[:], A.add, 256, [kb, W("TW")], [("SW", c.start, c.stop)])
+        tt(T.SL[:, c], T.TW[:], T.KEY1[:, 0:256], A.subtract, 256, [kb, W("TW")], [("SL", c.start, c.stop)])
 
     def square(sl):
         r = sl.start, sl.stop
@@ -423,21 +413,22 @@ def build(core, T, topo):
 
     def gather_headings(t):
         n = 1024 + 256 * t
-        for k0, kn, eng in CHUNKS:
+        for k0, kn, _, eng in CHUNKS:
             c, w = 256 * t + 16 * k0, 16 * kn
-            src = T.HT[:, 0:n].indirect(T.LT[:, c:c + w])
-            rd = [("HT", 0, n), ("LT", c, c + w)]
-            if eng == "V":
-                x = "XV%d" % nxt("x", 4)
-                cp(T[x][:, 0:16 * w], src, 16 * w * GC, rd, [W(x)])
-            else:
-                x = "GS%d" % nxt("s", 4)
-                act(T[x][:, 0:16 * w], src, F.Copy, 16 * w * GC, rd, [W(x)])
+            x = "XV%d" % nxt("x", 4) if eng == "V" else "GS%d" % nxt("s", 4)
+            for u, o in pieces(16 * w, c):
+                src, m = T.HT[:, 0:n].indirect(T.LT[:, o]), (u.stop - u.start) * GC
+                rd, wr = [("HT", 0, n), ("LT", o.start, o.stop)], [(x, u.start, u.stop)]
+                if eng == "V":
+                    cp(T[x][:, u], src, m, rd, wr)
+                else:
+                    act(T[x][:, u], src, F.Copy, m, rd, wr)
             bank = "B%d" % nxt("b", 3)
-            extract(bank, 0, [("E1", x)], True, True, w)
+            extract(bank, 0, "E1", x, True, True, w)
             sl = slice(16 * k0, 16 * k0 + w)
             cp(T.CL0[:, sl], T[bank][:, 0:w], w, [(bank, 0, w)], [("CL0", sl.start, sl.stop)])
-            ts(T.C32[:, sl], T[bank][:, 0:w], 32.0, A.mult, w, [(bank, 0, w)], [("C32", sl.start, sl.stop)], float(-OFF), A.add)
+            act(T.C32[:, sl], T[bank][:, 0:w], F.Identity, w, [(bank, 0, w), MOFF], [("C32", sl.start, sl.stop)],
+                bias=T.PF[:, 7:8], scale=32.0)
             square(sl)
 
     def visits(t):
@@ -446,31 +437,33 @@ def build(core, T, topo):
             nb, cl, cln = "NB%d" % a, "CL%d" % (a % 2), "CL%d" % (1 - a % 2)
             if a > 0 and t > 0:
                 apply_update(t - 1, a)
-            for k0, kn, eng in CHUNKS:
+            for k0, kn, eng, _ in CHUNKS:
                 w = 16 * kn
                 e16 = 16 * w
                 sl = slice(16 * k0, 16 * k0 + w)
                 bank = "B%d" % nxt("b", 3)
-                src = T[nb][:, 0:H].indirect(T[cl][:, sl])
+                win = T[nb][:, 0:H]
 
                 def C(n):
                     return (n, sl.start, sl.stop)
                 if eng == "V":
                     x, kb = "XV%d" % nxt("x", 4), "KV"
-                    tt(T[x][:, 0:e16], src, T[fv][:, 0:e16], A.is_lt, e16 * GC, [(nb, 0, H), C(cl), W(fv)], [W(x)])
-                    extract(bank, 0, [("E1", x)], True, True, w)
+                    for u, o in pieces(e16, sl.start):
+                        tt(T[x][:, u], win.indirect(T[cl][:, o]), T[fv][:, u], A.is_lt, (u.stop - u.start) * GC,
+                           [(nb, 0, H), (cl, o.start, o.stop), W(fv)], [(x, u.start, u.stop)])
+                    extract(bank, 0, "E1", x, True, True, w)
                 else:
                     j = nxt("s", 4)
                     x, s, kb = "GS%d" % j, "SS%d" % j, "KW"
-                    act(T[x][:, 0:e16], src, F.Copy, e16 * GC, [(nb, 0, H), C(cl)], [W(x)])
-                    for hh in range(2):
-                        u = slice(512 * hh, min(e16, 512 * hh + 512))
-                        m = u.stop - u.start
+                    for u, o in pieces(e16, sl.start):
+                        act(T[x][:, u], win.indirect(T[cl][:, o]), F.Copy, (u.stop - u.start) * GC,
+                            [(nb, 0, H), (cl, o.start, o.stop)], [(x, u.start, u.stop)])
+                    for hh, (u, _) in enumerate(pieces(e16, 0)):
                         db = "B%d" % (3 + hh)
-                        mms([(T[db][:, 0:m], T.ID[:], T[fv][:, u], True, False, m), (T[db][:, 0:m], T.IDN[:], T[x][:, u], False, True, m)],
-                            [W("ID"), W("IDN"), W(fv), W(x)], [W(db)])
-                        last = act(T[s][:, u], T[db][:, 0:m], F.Sign, m, [W(db), HLF], [(s, u.start, u.stop)], bias=T.PF[:, 6:7])
-                    extract(bank, 0, [("E05", s)], True, True, w)
+                        subtract(db, fv, u, x)
+                        act(T[s][:, u], T[db][:, 0:u.stop - u.start], F.Sign, u.stop - u.start, [W(db), HLF], [(s, u.start, u.stop)],
+                            bias=T.PF[:, 6:7])
+                    extract(bank, 0, "E05", s, True, True, w)
                 P, pr, kc = T[bank][:, 0:w], (bank, 0, w), 4 * t + a
                 ts(P, P, float(SLOPE), A.mult, w, [pr, (kb, kc, kc + 1)], [pr], T[kb][:, kc:kc + 1], A.add)
                 tt(P, P, T.SQ[:, sl], A.add, w, [pr, C("SQ")], [pr])
@@ -482,27 +475,24 @@ def build(core, T, topo):
                     square(sl)
                 else:
                     cp(T.CW[:, sl], T.CI[:, sl], w, [C("CI")], [C("CW")])
-        return last
 
     def election(t):
-        key = "KEY%d" % (t % 2)
-        C2 = ("B2", 0, 256)
+        C2, kr, z = ("B2", 0, 256), ("KEY0", 0, 256), slice(256 * t, 256 * t + 256)
         act(T.B2[:, 0:256], T.CW[:, 0:256], F.Copy, 256, [("CW", 0, 256)], [C2])
         act(T.CW[:, 256:384], T.CW[:, 0:128], F.Copy, 128, [("CW", 0, 128)], [("CW", 256, 384)])
 
         def K(a, b):
-            return T[key][:, a:b]
+            return T.KEY0[:, a:b]
         for d in range(1, 9):
             n, s, e = (256 if d < 8 else 128), 16 * d, ("EQ", 256 * d, 256 * d + 256)
             tt(T.EQ[:, d, 0:n], T.B2[:, 0:n], T.CW[:, s:s + n], A.is_equal, n, [C2, ("CW", s, s + n)], [e])
-            lst = [(K(0, n), T.IDK[:], T.EQ[:, d, 0:n], False, False, n),
+            lst = [(K(0, n), T.IDK[:], T.EQ[:, d, 0:n], d == 1, False, n),
                    (K(s, 256), T.IDK[:], T.EQ[:, d, 0:256 - s], False, d == 8, 256 - s)]
             if d < 8:
                 lst.append((K(0, s), T.IDK[:], T.EQ[:, d, 256 - s:256], False, False, s))
-            mms(lst, [e, W("IDK")], [(key, 0, 256)])
-        kr = (key, 0, 256)
-        tt(T.KK[:, 256:512], T.TW[:], K(0, 256), A.subtract, 256, [W("TW"), kr], [("KK", 256, 512)])
-        tt(T.KK[:, 0:256], K(0, 256), T.TW[:], A.add, 256, [W("TW"), kr], [("KK", 0, 256)])
+            mms(lst, [e, W("IDK")], [kr])
+        tt(T.KK[:, 256:512], T.SL[:, z], K(0, 256), A.subtract, 256, [("SL", z.start, z.stop), kr], [("KK", 256, 512)])
+        tt(T.KK[:, 0:256], K(0, 256), T.SW[:, z], A.add, 256, [("SW", z.start, z.stop), kr], [("KK", 0, 256)])
 
         def tree(src, w, out, oc):
             n, s, so = 128, src, 256 * w
@@ -531,12 +521,9 @@ def build(core, T, topo):
         for n in ("LF", "LU"):
             cp(T[n][:], T.WLI[:, 16:32], 16, [("WLI", 16, 32)], [W(n)])
 
-    def headings_out(t):
-        lst = []
-        for i in range(16):
-            for d in (0, 1):
-                lst.append((T.B0[:, i:256:16], sel(i, d), T.SPB[:, 16 * d:16 * d + 16], d == 0, d == 1, 16))
-        mms(lst, [("SPB", 0, 32), W("MIP")], [("B0", 0, 256)])
+    def headings_out(t, soft=()):
+        mms([(T.B0[:, i:256:16], sel(i, d), T.SPB[:, 16 * d:16 * d + 16], d == 0, d == 1, 16) for i in range(16) for d in (0, 1)],
+            [("SPB", 0, 32), W("MIP")], [("B0", 0, 256)], soft)
         c = 1024 + 256 * t
         act(T.HT[:, c:c + 256], T.B0[:, 0:256], F.Copy, 256, [("B0", 0, 256)], [("HT", c, c + 256)])
 
@@ -556,11 +543,8 @@ def build(core, T, topo):
         mms([(T.B4[:, 0:256], T.ID[:], T.OLD[:], True, False, 256), (T.B4[:, 0:256], T.ID[:], T.DC[:], False, True, 256)],
             [W("ID"), W("OLD"), W("DC")], [b4])
         act(T[ov][:, 0:256], T.B4[:, 0:256], F.Copy, 256, [b4], [(ov, 0, 256)])
-        lst = []
-        for i in range(16):
-            for d in (0, 1):
-                lst.append((T.B1[:, i:256:16], T.BI[:, 128 * i:128 * i + 128], T.SPB[:, 32 + 16 * d:48 + 16 * d], d == 0, d == 1, 16))
-        mms(lst, [("SPB", 32, 64), W("BI")], [b1])
+        mms([(T.B1[:, i:256:16], T.BI[:, 128 * i:128 * i + 128], T.SPB[:, 32 + 16 * d:48 + 16 * d], d == 0, d == 1, 16)
+             for i in range(16) for d in (0, 1)], [("SPB", 32, 64), W("BI")], [b1])
         cp(T.LB[:], T.B1[:, 0:256], 256, [b1], [W("LB")])
         for lo in (0, 8):
             er = ("EQT", 256 * lo, 256 * lo + 2048)
@@ -585,8 +569,8 @@ def build(core, T, topo):
 
     def bias(t, a, src):
         c = 4 * (t + 1) + a
-        for kb, v in (("KV", BV), ("KW", BS)):
-            ts(T[kb][:, c:c + 1], T[src][:, 256:257], 32.0, A.mult, 1, [(src, 256, 257)], [(kb, c, c + 1)], float(v), A.add)
+        for kb in ("KV", "KW"):
+            act(T[kb][:, c:c + 1], T[src][:, 256:257], F.Identity, 1, [(src, 256, 257), (kb, 0, 1)], [(kb, c, c + 1)], bias=T[kb][:, 0:1], scale=32.0)
 
     def kappa(t):
         ov = "OUTV%d" % t
@@ -615,30 +599,32 @@ def build(core, T, topo):
         iv, il = "INV%d_%d" % (a, t), "INL%d_%d" % (a, t)
         src = (rank + a) % NR
         for nm, sm in ((il, "il%d_%d"), (iv, "iv%d_%d")):
-            add(gr, "R", None, 0.0, [], [W(nm)], "r", sm % (src, t), len(cross), 3.5, soft=[sent[t]])
+            gr["nodes"][add(gr, "R", None, 0.0, [], [W(nm)], "r", sm % (src, t), len(cross), 3.5)]["soft"].add(sent[t])
         bias(t, a, iv)
         scatter("NB%d" % a, iv, il)
 
     lists(0)
     permute(0)
     gather_headings(0)
-    shares(0, SHARE0)
     first_v = len(gr["nodes"]) - 1
     lists(1)
+    shares(0)
     for t in range(1, RT):
         permute(t)
-        load_tiles(t, "Y", [first_v])
+        load_tiles(t, [first_v])
+        shares(t)
     for t in range(RT):
-        last = visits(t)
-        if t + 1 < RT:
-            shares(t + 1, (), [last])
+        visits(t)
         election(t)
-        headings_out(t)
-        notes(t)
         if t + 1 < RT:
+            headings_out(t)
+            notes(t)
             gather_headings(t + 1)
             kappa(t)
             send_update(t)
+        else:
+            notes(t)
+            headings_out(t, [len(gr["nodes"]) - 1])
         write_yh(t)
     for j, e in ((0, "S"), (1, "Y")):
         dma(e, T.yl[:, HALF * j:HALF * j + HALF], T.NB0[:, HALF * j:HALF * j + HALF], 5.0, [("NB0", HALF * j, HALF * j + HALF)], [])

from concourse.bass import DstId, RemoteDMATransfer
from concourse.mybir import AluOpType as A, ActivationFunctionType as F

NR, RT, H, DUMMY, HALF = 4, 4, 4096, 256, 2048
MOD = 131072
KS = 130
SLOPE = 613 * 32 + MOD * KS
OFF = MOD * 512
BV = -256 - MOD * (9 * KS + 1) - OFF
BS = BV + 8 * SLOPE
CHUNKS = ((0, 4, "V", "V"), (4, 4, "S", "S"), (8, 5, "V", "S"), (13, 3, "S", "S"))
SHARE_V = (0, 2)
PIECE = 512
CYC, GC, PEC = 0.83e-3 * 1.25, 1.56, 0.68e-3

SCRATCH = {}
SEMAPHORES = ["cv", "cs", "cp", "cg", "lsend"] + ["d%d" % j for j in range(52)] + ["ls%d" % j for j in range(10)]


def _buf(names, cols, dtype, where="sbuf", rows=128):
    for n in names.split():
        SCRATCH[n] = (where, [rows] + (cols if isinstance(cols, list) else [cols]), dtype)


B16, F32, I32, U16 = "bfloat16", "float32", "int32", "uint16"
_buf("NB0 NB1 NB2 NB3", H + DUMMY, B16)
_buf("FE HT", 2048, B16)
_buf("FVT0 FVT1 FVT2 FVT3 XV0 XV1 XV2 XV3 GS0 GS1 GS2 GS3", 1280, B16)
_buf("OUTV0 OUTV1 OUTV2 OUTV3", 264, B16)
_buf("OUTL0 OUTL1 OUTL2 OUTL3 LU", 16, U16)
for _t in range(RT - 1):
    for _a in range(NR):
        SEMAPHORES += ["iv%d_%d" % (_a, _t), "il%d_%d" % (_a, _t)]
        if _a:
            _buf("INV%d_%d" % (_a, _t), 264, B16)
            _buf("INL%d_%d" % (_a, _t), 16, U16)
for _a in range(1, NR):
    SEMAPHORES += ["n%d_0" % _a, "n%d_1" % _a]
_buf("ZL ZR", [32, 16], I32)
_buf("Z ZT", [32, 32], I32)
_buf("LT", 1024, U16)
_buf("HD SPI", 64, I32)
_buf("HDI", 128, I32)
_buf("HDB BMW ID IDN IDK ONES", 128, B16)
_buf("RI", 160, F32)
_buf("RG", 128, F32)
_buf("PI PM PG KI KJ", 2, I32)
_buf("PF", 8, F32)
_buf("MK DUP KV KW LF DL OF", 16, F32)
_buf("MB", 160, B16)
_buf("MIP", 16 * 160, B16)
_buf("BI", 16 * 128, B16)
_buf("E1 E05 ES1 ES5 ESN EX", 144, B16)
_buf("FL OLD DC", 256, B16)
_buf("SW SL", 1024, F32)
_buf("TW C32 SQ M1", 256, F32)
_buf("TRI", [16, 16], B16)
_buf("SS0 SS1 SS2 SS3 XH0 XH1 GH0 GH1 SH0 SH1", 1024, B16)
_buf("CL0 CL1 LB", 256, U16)
_buf("TI CI", 256, I32)
_buf("CW", 384, F32)
_buf("EQ", [9, 256], B16)
_buf("EQT", [16, 256], B16)
_buf("KK DD", 512, F32)
_buf("M2", 128, F32)
_buf("M3", 64, F32)
_buf("WLI", 32, I32)
_buf("SPB", 64, B16)
_buf("KS1", 2, F32)
_buf("JUNK", 32, F32)
_buf("YH8", 1024, F32, rows=8)
_buf("B0 B1 B2 B3 B4 B5 KEY0 KEY1", 512, F32, "psum")
PSUM = set(n for n in SCRATCH if SCRATCH[n][0] == "psum")
CSEM = {"V": "cv", "S": "cs", "P": "cp", "G": "cg"}


def add(gr, eng, emit, cost, reads=(), writes=(), kind="c", sem=None, val=0, lat=0.0, est=0.0, soft=()):
    nodes = gr["nodes"]
    i = len(nodes)
    deps = set()
    for w, regs in ((0, reads), (1, writes)):
        for (b, c0, c1) in regs:
            if b in PSUM:
                st = gr["bank"].setdefault(b, [[], [], None])
                if st[2] != eng:
                    st[0], st[1], st[2] = st[1], [], eng
                deps.update(e[0] for e in st[0])
                deps.update(j for (j, d0, d1, dw) in st[1] if d0 < c1 and c0 < d1 and (w or dw))
                st[1].append((i, c0, c1, w))
            else:
                keep = []
                for e in gr["acc"].get(b, []):
                    j, d0, d1, dw = e
                    if d0 < c1 and c0 < d1 and (w or dw):
                        deps.add(j)
                    if not (w and j != i and c0 <= d0 and d1 <= c1):
                        keep.append(e)
                gr["acc"][b] = keep + [(i, c0, c1, w)]
    deps.discard(i)
    nodes.append({"id": i, "eng": eng, "emit": emit, "cost": cost, "kind": kind, "sem": sem, "val": val, "deps": deps,
                  "soft": set(soft) - deps, "lat": lat, "est": est, "done": (sem, val)})
    return i


def schedule(gr):
    nodes = gr["nodes"]
    succ = [[] for _ in nodes]
    for n in nodes:
        for j in n["deps"] | n["soft"]:
            succ[j].append(n["id"])
    rank = [0.0] * len(nodes)
    for n in reversed(nodes):
        rank[n["id"]] = max([0.0] + [rank[s] for s in succ[n["id"]]]) + n["cost"] + n["lat"] + 0.05
    left = [len(n["deps"] | n["soft"]) for n in nodes]
    at = [n["est"] for n in nodes]
    free, ready = {"R": 0.0}, {}
    for n in nodes:
        free[n["eng"]] = 0.0
        ready.setdefault(n["eng"], set())
        if left[n["id"]] == 0:
            ready[n["eng"]].add(n["id"])
    order = []
    while len(order) < len(nodes):
        best = None
        for e in ready:
            if ready[e]:
                s = max(free[e], min(at[i] for i in ready[e]))
                if best is None or s < best[0]:
                    best = (s, e)
        s, e = best
        i = max((k for k in ready[e] if at[k] <= s), key=lambda k: (rank[k], -k))
        n = nodes[i]
        ready[e].discard(i)
        if e != "R":
            free[e] = s + n["cost"]
        order.append(i)
        for k in succ[i]:
            left[k] -= 1
            at[k] = max(at[k], s + n["cost"] + (n["lat"] if i in nodes[k]["deps"] else 0.0))
            if left[k] == 0:
                ready[nodes[k]["eng"]].add(k)
    return order


def emit_all(gr, order, g, T):
    q = {"V": g.vector, "S": g.scalar, "P": g.tensor, "G": g, "Y": g.sync}
    nodes, clk = gr["nodes"], {}
    known = dict((e, {}) for e in q)
    final = {}
    for i in order:
        n = nodes[i]
        if n["kind"] == "r":
            final[n["sem"]] = n["val"]
            continue
        e = n["eng"]
        cl = dict(known[e])
        need = {}
        for j in n["deps"]:
            d = nodes[j]
            if not (e == "P" and d["eng"] == "P"):
                s, v = d["done"]
                need[s] = max(need.get(s, 0), v)
        items = sorted(need.items(), key=lambda x: (-x[1], x[0]))
        for s, v in items:
            if cl.get(s, 0) >= v or any(s2 != s and clk.get((s2, v2), {}).get(s, 0) >= v and known[e].get(s2, 0) < v2
                                        for s2, v2 in items):
                continue
            q[e].wait_ge(T.sem[s], int(v))
            cl[s] = v
            for s3, v3 in clk.get((s, v), {}).items():
                cl[s3] = max(cl.get(s3, 0), v3)
        known[e] = cl
        ins = n["emit"](q[e])
        if n["kind"] == "c":
            s = CSEM[e]
            n["done"] = (s, final.get(s, 0) + 1)
            ins.then_inc(T.sem[s], 1)
        elif n["kind"] == "d":
            ins.then_inc(T.sem[n["sem"]], 16)
        final[n["done"][0]] = max(final.get(n["done"][0], 0), n["done"][1])
        clk[n["done"]] = cl
    for s in sorted(final):
        if known["G"].get(s, 0) < final[s]:
            g.wait_ge(T.sem[s], int(final[s]))


def build(core, T, topo):
    rank = T.rank_of(core)
    gr = {"nodes": [], "acc": {}, "bank": {}}
    num = {"d": 0, "ls": 0, "x": 0, "s": 0, "b": 0, "lsend": 0}
    lastd = {}

    def nxt(k, n):
        num[k] += 1
        return (num[k] - 1) % n

    def W(n):
        return (n, 0, 1 << 20)

    def vec(fn, cyc, reads, writes):
        return add(gr, "V", fn, max(64, cyc) * CYC + 0.04, reads, writes)

    def gps(fn, cyc, writes):
        return add(gr, "G", fn, cyc * CYC + 0.15, [], writes)

    def dma(eng, out, in_, lat, reads, writes, soft=()):
        s = "d%d" % nxt("d", 99)
        lastd[eng] = add(gr, eng, lambda q: q.dma_start(out, in_), 0.06, reads, writes, "d", s, 16, lat,
                         soft=list(soft) + ([lastd[eng]] if eng in lastd else []))

    def tt(out, in0, in1, op, cyc, reads, writes):
        return vec(lambda q: q.tensor_tensor(out=out, in0=in0, in1=in1, op=op), cyc, reads, writes)

    def ts(out, in0, s1, op0, cyc, reads, writes, s2=None, op1=None):
        if op1 is None:
            return vec(lambda q: q.tensor_scalar(out=out, in0=in0, scalar1=s1, scalar2=None, op0=op0), cyc, reads, writes)
        return vec(lambda q: q.tensor_scalar(out=out, in0=in0, scalar1=s1, scalar2=s2, op0=op0, op1=op1), cyc, reads, writes)

    def cp(out, in_, cyc, reads, writes):
        return vec(lambda q: q.tensor_copy(out=out, in_=in_), cyc, reads, writes)

    def fill(ap, val, n, reg):
        vec(lambda q: q.memset(ap, val), n, [], [reg])

    def act(out, in_, func, cyc, reads, writes, bias=0.0, scale=1.0, accum=None, soft=()):
        def f(q):
            if accum is not None:
                return q.activation(out=out, in_=in_, func=func, bias=bias, scale=scale, accum_out=accum)
            return q.activation(out=out, in_=in_, func=func, bias=bias, scale=scale)
        return add(gr, "S", f, max(64, cyc) * CYC + 0.1, reads, writes, soft=soft)

    def mms(lst, reads, writes, soft=()):
        def f(q):
            for (o, l, r, st, sp, _) in lst:
                ins = q.matmul(o, l, r, st, sp)
            return ins
        return add(gr, "P", f, sum(max(64, x[5]) for x in lst) * PEC + 0.03, reads, writes, soft=soft)

    def extract(bank, c0, en, x, start, stop, n=64, reg=None):
        return mms([(T[bank][:, c0:c0 + n], T[en][:, 15 - i:143 - i], T[x][:, i:16 * n:16], start and i == 0, stop and i == 15, n)
                    for i in range(16)], [(x, 0, 16 * n), W(en)], [reg or (bank, c0, c0 + n)])

    def pieces(n, c):
        return [(slice(j, min(n, j + PIECE)), slice(c + j // 16, c + min(n, j + PIECE) // 16)) for j in range(0, n, PIECE)]

    def subtract(bank, fv, u, x):
        m = u.stop - u.start
        mms([(T[bank][:, 0:m], T.ID[:], T[fv][:, u], True, False, m)], [W("ID"), W(fv)], [W(bank)])
        mms([(T[bank][:, 0:m], T.IDN[:], T[x][:, u], False, True, m)], [W("IDN"), (x, u.start, u.stop)], [W(bank)])

    dma("S", T.HD[:], T.hd[:], 2.2, [], [W("HD")])
    for a in range(4):
        for h in range(2):
            r0 = 32 * a + 16 * h
            for e, n, d in (("S", "ZL", 0), ("Y", "ZR", 16)):
                dma(e, T[n][r0:r0 + 16], T.comp[32 * a + d:32 * a + d + 16, 512 * h:512 * h + 512], 6.5, [], [(n, r0, r0 + 1)])
    for h in (0, 1):
        dma("Y", T.NB0[:, HALF * h:HALF * h + HALF], T.lim[:, HALF * h:HALF * h + HALF], 11.0, [], [("NB0", HALF * h, HALF * h + HALF)])
    dma("S", T.FVT0[:, 0:256], T.feat[:, 1024:1280], 13.0, [], [("FVT0", 0, 256)])
    dma("S", T.FE[:], T.feat[:], 16.0, [], [W("FE")])

    def load_tiles(t, soft):
        for j in range(5):
            dma("Y", T["FVT%d" % t][:, 256 * j:256 * j + 256], T.feat[:, 1024 + 256 * t:1280 + 256 * t],
                4.0, [], [("FVT%d" % t, 256 * j, 256 * j + 256)], soft)

    gps(lambda q: q.iota(T.PI[:, 0:1], [[1, 1]], 0, 1), 2, [W("PI")])
    for n, pat, base, c in (("RI", [[1, 160]], 0, 320), ("RG", [[16, 8], [0, 16]], 0, 256),
                            ("TW", [[-4096, 16], [0, 16]], 15 * 4096, 512), ("DUP", [[16, 16]], H, 32)):
        gps(lambda q, n=n, pat=pat, base=base: q.iota(T[n][:], pat, base, 0, allow_small_or_imprecise_dtypes=True), c, [W(n)])
    ts(T.PM[:, 0:1], T.PI[:, 0:1], 15, A.bitwise_and, 1, [W("PI")], [W("PM")])
    ts(T.PG[:, 0:1], T.PI[:, 0:1], 112, A.bitwise_and, 1, [W("PI")], [W("PG")])
    for c, s, d in ((0, "PI", 0), (1, "PM", 0), (2, "PG", 0), (3, "PI", 16), (4, "PG", 15)):
        ts(T.PF[:, c:c + 1], T[s][:, 0:1], d, A.add, 1, [W(s)], [("PF", c, c + 1)])
    for c, v in ((5, OFF // 32 + 16), (6, -0.5), (7, -OFF)):
        fill(T.PF[:, c:c + 1], float(v), 1, ("PF", c, c + 1))
    SQB, HLF, MOFF = ("PF", 5, 6), ("PF", 6, 7), ("PF", 7, 8)

    def eqc(name, n, col, val, src="RI"):
        ts(T[name][:, 0:n], T[src][:, 0:n], T.PF[:, col:col + 1], A.is_equal, n, [W(src), ("PF", col, col + 1)], [W(name)], val, A.mult)
    eqc("MB", 160, 3, 1.0)
    eqc("MK", 16, 1, 1.0)
    for y in range(16):
        act(T.MIP[:, 160 * y:160 * y + 160], T.MB[:], F.Copy, 160, [W("MB"), W("MK")], [("MIP", 160 * y, 160 * y + 160)],
            scale=T.MK[:, y:y + 1], soft=[lastd["S"]])
    for n, v in (("E1", 1.0), ("ES1", 65536.0), ("E05", 0.5), ("EX", 0.0625), ("ES5", 32768.0), ("ESN", -32768.0)):
        eqc(n, 144, 4, v)
    for n, v in (("ID", 1.0), ("IDN", -1.0), ("IDK", float(1 << 28))):
        eqc(n, 128, 0, v)
    eqc("BMW", 128, 2, 1.0, "RG")
    ts(T.DUP[:], T.DUP[:], T.PF[:, 1:2], A.add, 16, [W("DUP"), ("PF", 1, 2)], [W("DUP")])
    for y in range(16):
        act(T.BI[:, 128 * y:128 * y + 128], T.BMW[:], F.Copy, 128, [W("BMW"), W("MK")], [("BI", 128 * y, 128 * y + 128)],
            scale=T.MK[:, y:y + 1], soft=[lastd["S"]])
        ts(T.TRI[:, y, :], T.RI[:, 0:16], T.PF[:, 1:2], A.is_gt, 16, [W("RI"), ("PF", 1, 2)], [("TRI", 16 * y, 16 * y + 16)])
    fill(T.ONES[:], 1.0, 64, W("ONES"))
    fill(T.KV[:, 0:4], float(BV), 4, ("KV", 0, 4))
    fill(T.KW[:, 0:4], float(BS), 4, ("KW", 0, 4))
    for t in range(RT - 1):
        fill(T["OUTV%d" % t][:, 256:264], 0.0, 4, ("OUTV%d" % t, 256, 264))
    for c0, c1, w in ((256, 512, 256), (512, 1024, 512), (1024, 1280, 256)):
        cp(T.FVT0[:, c0:c1], T.FVT0[:, 0:w], w // 2, [("FVT0", 0, w)], [("FVT0", c0, c1)])

    ts(T.HDI[:, 0:64], T.HD[:], 4080, A.bitwise_and, 64, [W("HD")], [("HDI", 0, 64)])
    ts(T.HDI[:, 64:128], T.HD[:], 15, A.bitwise_and, 64, [W("HD")], [("HDI", 64, 128)])
    cp(T.HDB[:], T.HDI[:], 128, [W("HDI")], [W("HDB")])

    def sel(i, d):
        return T.MIP[:, 160 * i + 16 + i - d:160 * i + 144 + i - d]
    for b in range(2):
        bank = "B%d" % b
        mms([(T[bank][:, 64 * y:64 * y + 64], sel(8 * b + y, d), T.HDB[:, 64 * d:64 * d + 64], d == 0, d == 1, 64)
             for y in range(8) for d in (0, 1)], [W("MIP"), W("HDB")], [(bank, 0, 512)])
        act(T.HT[:, 512 * b:512 * b + 512], T[bank][:], F.Copy, 512, [(bank, 0, 512)], [("HT", 512 * b, 512 * b + 512)])

    def lists(tp):
        b0 = 16 * tp
        zr = ("Z", 32 * b0, 32 * b0 + 512)
        cp(T.Z[:, b0:b0 + 16, 0:16], T.ZL[:, b0:b0 + 16, :], 256, [W("ZL")], [zr])
        cp(T.Z[:, b0:b0 + 16, 16:32], T.ZR[:, b0:b0 + 16, :], 256, [W("ZR")], [zr])
        for b in range(b0, b0 + 16):
            vec(lambda q, b=b: q.transpose(T.ZT[:, :, b], T.Z[:, b, :]), 32, [zr], [("ZT", 512 * tp, 512 * tp + 512)])

    def permute(t):
        tp, h = t % 2, t // 2
        cp(T.LT[:, 256 * t:256 * t + 256], T.ZT[:, 16 * h:16 * h + 16, 16 * tp:16 * tp + 16], 256,
           [("ZT", 512 * tp, 512 * tp + 512)], [("LT", 256 * t, 256 * t + 256)])

    cores = T.cores

    def rel(src, dst):
        return (src - dst) % NR

    def addr(dst):
        return topo.addr(cores[dst])[0:2]
    onchip = [r for r in range(NR) if r != rank and topo.chip(cores[r]) == topo.chip(core)][0]
    far = [r for r in range(NR) if topo.chip(cores[r]) != topo.chip(core)]
    cross = topo.engines(core, cores[far[0]])
    local = [e for e in topo.engines(core, cores[onchip]) if e not in cross]
    wide = local + cross
    bulk = []

    def emask(es):
        return sum(1 << e for e in es)

    def send(src, h, dst, es):
        s = "ls%d" % nxt("ls", 99)
        rid, pid = addr(dst)
        buf = "NB%d" % rel(src, rank)
        out = T["NB%d" % rel(src, dst)][:, HALF * h:HALF * h + HALF]
        in_ = T[buf][:, HALF * h:HALF * h + HALF]
        rs = T.sem["n%d_%d" % (rel(src, dst), h)]
        bulk.append(add(gr, "G", lambda q: q.remote_dma(out, in_, rs, T.sem[s], pid, rid, emask(es)), 0.8,
                        [(buf, HALF * h, HALF * h + HALF)], [], "s", s, len(es), 6.0, soft=bulk[-1:]))

    def recv(src, h, est, n):
        a = rel(src, rank)
        add(gr, "R", None, 0.0, [], [("NB%d" % a, HALF * h, HALF * h + HALF)], "r", "n%d_%d" % (a, h), n, est=est)

    first = rank if (rank - 1) % NR in far else onchip
    o_first = [r for r in far if (r - 1) % NR not in far][0]
    o_second = [r for r in far if r != o_first][0]
    gate, mygate = (first - 1) % NR, (o_first - 1) % NR
    nown = len(wide) if rank == first else len(local)
    recv(onchip, 1, 10.0, nown)
    recv(onchip, 0, 14.0, nown)
    late = 0.0 if rank == mygate else 6.0
    nin = len(cross) if rank == mygate else len(wide)
    for src, e in ((o_first, 24.0), (o_second, 34.0)):
        for h in range(2):
            recv(src, h, e + late, nin)
    if rank == first:
        for h in range(2):
            send(rank, h, gate, cross)
        for h in range(2):
            send(rank, h, onchip, local)
    else:
        for h in range(2):
            send(rank, h, onchip, wide)
        for h in range(2):
            send(rank, h, gate, cross)
    if rank == mygate:
        for src in (o_first, o_second):
            for h in range(2):
                send(src, h, onchip, wide)

    def shares(t):
        fv, n, kb = "FVT%d" % t, 1024 + 256 * t, W("KEY1")
        for ch in sorted(range(4), key=lambda x: x not in SHARE_V):
            c = 256 * t + 64 * ch
            if ch in SHARE_V:
                x = "XH%d" % (ch // 2)
                tt(T[x][:], T.FE[:, 0:n].indirect(T.LT[:, c:c + 64]), T[fv][:, 0:1024], A.min, 1024 * GC,
                   [W("FE"), ("LT", c, c + 64), W(fv)], [W(x)])
                extract("KEY1", 64 * ch, "ES1", x, True, True, reg=kb)
            else:
                x, s = "GH%d" % (ch % 2), "SH%d" % (ch % 2)
                for u, o in pieces(1024, c):
                    act(T[x][:, u], T.FE[:, 0:n].indirect(T.LT[:, o]), F.Copy, (u.stop - u.start) * GC,
                        [W("FE"), ("LT", o.start, o.stop)], [(x, u.start, u.stop)])
                    subtract("B5", fv, u, x)
                    act(T[s][:, u], T.B5[:], F.Abs, u.stop - u.start, [W("B5")], [(s, u.start, u.stop)])
                extract("KEY1", 64 * ch, "ES5", fv, True, False, reg=kb)
                extract("KEY1", 64 * ch, "ES5", x, False, False, reg=kb)
                extract("KEY1", 64 * ch, "ESN", s, False, True, reg=kb)
        c = slice(256 * t, 256 * t + 256)
        tt(T.SW[:, c], T.KEY1[:, 0:256], T.TW[:], A.add, 256, [kb, W("TW")], [("SW", c.start, c.stop)])
        tt(T.SL[:, c], T.TW[:], T.KEY1[:, 0:256], A.subtract, 256, [kb, W("TW")], [("SL", c.start, c.stop)])

    def square(sl):
        r = sl.start, sl.stop
        act(T.SQ[:, sl], T.C32[:, sl], F.Square, r[1] - r[0], [("C32",) + r, SQB], [("SQ",) + r], bias=T.PF[:, 5:6], scale=1.0 / 32)

    def gather_headings(t):
        n = 1024 + 256 * t
        for k0, kn, _, eng in CHUNKS:
            c, w = 256 * t + 16 * k0, 16 * kn
            x = "XV%d" % nxt("x", 4) if eng == "V" else "GS%d" % nxt("s", 4)
            for u, o in pieces(16 * w, c):
                src, m = T.HT[:, 0:n].indirect(T.LT[:, o]), (u.stop - u.start) * GC
                rd, wr = [("HT", 0, n), ("LT", o.start, o.stop)], [(x, u.start, u.stop)]
                if eng == "V":
                    cp(T[x][:, u], src, m, rd, wr)
                else:
                    act(T[x][:, u], src, F.Copy, m, rd, wr)
            bank = "B%d" % nxt("b", 3)
            extract(bank, 0, "E1", x, True, True, w)
            sl = slice(16 * k0, 16 * k0 + w)
            cp(T.CL0[:, sl], T[bank][:, 0:w], w, [(bank, 0, w)], [("CL0", sl.start, sl.stop)])
            act(T.C32[:, sl], T[bank][:, 0:w], F.Identity, w, [(bank, 0, w), MOFF], [("C32", sl.start, sl.stop)],
                bias=T.PF[:, 7:8], scale=32.0)
            square(sl)

    def visits(t):
        fv = "FVT%d" % t
        for a in range(NR):
            nb, cl, cln = "NB%d" % a, "CL%d" % (a % 2), "CL%d" % (1 - a % 2)
            if a > 0 and t > 0:
                apply_update(t - 1, a)
            for k0, kn, eng, _ in CHUNKS:
                w = 16 * kn
                e16 = 16 * w
                sl = slice(16 * k0, 16 * k0 + w)
                bank = "B%d" % nxt("b", 3)
                win = T[nb][:, 0:H]

                def C(n):
                    return (n, sl.start, sl.stop)
                if eng == "V":
                    x, kb = "XV%d" % nxt("x", 4), "KV"
                    for u, o in pieces(e16, sl.start):
                        tt(T[x][:, u], win.indirect(T[cl][:, o]), T[fv][:, u], A.is_lt, (u.stop - u.start) * GC,
                           [(nb, 0, H), (cl, o.start, o.stop), W(fv)], [(x, u.start, u.stop)])
                    extract(bank, 0, "E1", x, True, True, w)
                else:
                    j = nxt("s", 4)
                    x, s, kb = "GS%d" % j, "SS%d" % j, "KW"
                    for u, o in pieces(e16, sl.start):
                        act(T[x][:, u], win.indirect(T[cl][:, o]), F.Copy, (u.stop - u.start) * GC,
                            [(nb, 0, H), (cl, o.start, o.stop)], [(x, u.start, u.stop)])
                    for hh, (u, _) in enumerate(pieces(e16, 0)):
                        db = "B%d" % (3 + hh)
                        subtract(db, fv, u, x)
                        act(T[s][:, u], T[db][:, 0:u.stop - u.start], F.Sign, u.stop - u.start, [W(db), HLF], [(s, u.start, u.stop)],
                            bias=T.PF[:, 6:7])
                    extract(bank, 0, "E05", s, True, True, w)
                P, pr, kc = T[bank][:, 0:w], (bank, 0, w), 4 * t + a
                ts(P, P, float(SLOPE), A.mult, w, [pr, (kb, kc, kc + 1)], [pr], T[kb][:, kc:kc + 1], A.add)
                tt(P, P, T.SQ[:, sl], A.add, w, [pr, C("SQ")], [pr])
                tt(T.TI[:, sl], P, T.C32[:, sl], A.max, w, [pr, C("C32")], [C("TI")])
                ts(T.CI[:, sl], T.TI[:, sl], 5, A.arith_shift_right, w, [C("TI")], [C("CI")], 4095, A.bitwise_and)
                if a < NR - 1:
                    cp(T[cln][:, sl], T.CI[:, sl], w, [C("CI")], [C(cln)])
                    ts(T.C32[:, sl], T.CI[:, sl], 32.0, A.mult, w, [C("CI")], [C("C32")], float(-OFF), A.add)
                    square(sl)
                else:
                    cp(T.CW[:, sl], T.CI[:, sl], w, [C("CI")], [C("CW")])

    def election(t):
        C2, kr, z = ("B2", 0, 256), ("KEY0", 0, 256), slice(256 * t, 256 * t + 256)
        act(T.B2[:, 0:256], T.CW[:, 0:256], F.Copy, 256, [("CW", 0, 256)], [C2])
        act(T.CW[:, 256:384], T.CW[:, 0:128], F.Copy, 128, [("CW", 0, 128)], [("CW", 256, 384)])

        def K(a, b):
            return T.KEY0[:, a:b]
        for d in range(1, 9):
            n, s, e = (256 if d < 8 else 128), 16 * d, ("EQ", 256 * d, 256 * d + 256)
            tt(T.EQ[:, d, 0:n], T.B2[:, 0:n], T.CW[:, s:s + n], A.is_equal, n, [C2, ("CW", s, s + n)], [e])
            lst = [(K(0, n), T.IDK[:], T.EQ[:, d, 0:n], d == 1, False, n),
                   (K(s, 256), T.IDK[:], T.EQ[:, d, 0:256 - s], False, d == 8, 256 - s)]
            if d < 8:
                lst.append((K(0, s), T.IDK[:], T.EQ[:, d, 256 - s:256], False, False, s))
            mms(lst, [e, W("IDK")], [kr])
        tt(T.KK[:, 256:512], T.SL[:, z], K(0, 256), A.subtract, 256, [("SL", z.start, z.stop), kr], [("KK", 256, 512)])
        tt(T.KK[:, 0:256], K(0, 256), T.SW[:, z], A.add, 256, [("SW", z.start, z.stop), kr], [("KK", 0, 256)])

        def tree(src, w, out, oc):
            n, s, so = 128, src, 256 * w
            for m in ("M1", "M2", "M3", None):
                dst, do = (out, oc) if m is None else (m, n * w)
                tt(T[dst][:, do:do + n], T[s][:, so:so + n], T[s][:, so + n:so + 2 * n], A.max, 2 * n, [(s, so, so + 2 * n)], [(dst, do, do + n)])
                n, s, so = n // 2, dst, do
        tree("KK", 1, "B4", 0)
        tree("KK", 0, "B3", 0)
        n = 16
        while n < 256:
            for b in ("B4", "B3"):
                cp(T[b][:, n:2 * n], T[b][:, 0:n], n, [(b, 0, n)], [(b, n, 2 * n)])
            n *= 2
        for b, w in (("B4", 1), ("B3", 0)):
            c = slice(256 * w, 256 * w + 256)
            q = ("DD", c.start, c.stop)
            tt(T.DD[:, c], T.KK[:, c], T[b][:, 0:256], A.subtract, 256, [("KK", c.start, c.stop), (b, 0, 256)], [q])
            tt(T.DD[:, c], T.DD[:, c], T.B2[:, 0:256], A.add, 256, [q, C2], [q])
            tree("DD", w, "WLI", 16 * w)
        for w in (1, 0):
            rd, o = ("WLI", 16 * w, 16 * w + 16), 32 * w
            for d, m in ((0, 4080), (16, 15)):
                ts(T.SPI[:, o + d:o + d + 16], T.WLI[:, 16 * w:16 * w + 16], m, A.bitwise_and, 16, [rd], [("SPI", o + d, o + d + 16)])
            cp(T.SPB[:, o:o + 32], T.SPI[:, o:o + 32], 32, [("SPI", o, o + 32)], [("SPB", o, o + 32)])
        for n in ("LF", "LU"):
            cp(T[n][:], T.WLI[:, 16:32], 16, [("WLI", 16, 32)], [W(n)])

    def headings_out(t, soft=()):
        mms([(T.B0[:, i:256:16], sel(i, d), T.SPB[:, 16 * d:16 * d + 16], d == 0, d == 1, 16) for i in range(16) for d in (0, 1)],
            [("SPB", 0, 32), W("MIP")], [("B0", 0, 256)], soft)
        c = 1024 + 256 * t
        act(T.HT[:, c:c + 256], T.B0[:, 0:256], F.Copy, 256, [("B0", 0, 256)], [("HT", c, c + 256)])

    def write_yh(t):
        c, y = 1024 + 256 * t, ("YH8", 256 * t, 256 * t + 256)
        mms([(T.B5[0:8, 0:256], T.BMW[:, 0:128:16], T.HT[:, c:c + 256], True, True, 256)], [W("BMW"), ("HT", c, c + 256)], [("B5", 0, 256)])
        act(T.YH8[:, 256 * t:256 * t + 256], T.B5[0:8, 0:256], F.Copy, 256, [("B5", 0, 256)], [y])
        dma("Y", T.yh[:, 256 * t:256 * t + 256], T.YH8[:, 256 * t:256 * t + 256], 2.5, [y], [])

    def notes(t):
        fv, ov, ol = "FVT%d" % t, "OUTV%d" % t, "OUTL%d" % t
        b1, b3, b4 = ("B1", 0, 256), ("B3", 0, 256), ("B4", 0, 256)
        act(T.OLD[:], T.NB0[:, 0:H].indirect(T.LU[:, 0:16]), F.Copy, 256 * GC, [("NB0", 0, H), W("LU")], [W("OLD")])
        mms([(T.B3[:, 0:256], T.ID[:], T[fv][:, 0:256], True, False, 256), (T.B3[:, 0:256], T.IDN[:], T.OLD[:], False, True, 256)],
            [W("ID"), W("IDN"), W(fv), W("OLD")], [b3])
        ts(T.DC[:], T.B3[:, 0:256], 32.0, A.min, 256, [b3], [W("DC")], -32.0, A.max)
        mms([(T.B4[:, 0:256], T.ID[:], T.OLD[:], True, False, 256), (T.B4[:, 0:256], T.ID[:], T.DC[:], False, True, 256)],
            [W("ID"), W("OLD"), W("DC")], [b4])
        act(T[ov][:, 0:256], T.B4[:, 0:256], F.Copy, 256, [b4], [(ov, 0, 256)])
        mms([(T.B1[:, i:256:16], T.BI[:, 128 * i:128 * i + 128], T.SPB[:, 32 + 16 * d:48 + 16 * d], d == 0, d == 1, 16)
             for i in range(16) for d in (0, 1)], [("SPB", 32, 64), W("BI")], [b1])
        cp(T.LB[:], T.B1[:, 0:256], 256, [b1], [W("LB")])
        for lo in (0, 8):
            er = ("EQT", 256 * lo, 256 * lo + 2048)
            for mb in range(lo, lo + 8):
                n = 256 - 16 * mb
                ts(T.EQT[:, mb, 0:n], T.LB[:, 16 * mb:256], T.LF[:, mb:mb + 1], A.is_equal, n * 0.5, [W("LB"), W("LF")], [("EQT", 256 * mb, 256 * mb + 256)])
            tt(T.EQT[:, lo:lo + 8, 0:16], T.EQT[:, lo:lo + 8, 0:16], T.TRI[:, lo:lo + 8, :], A.mult, 256, [er, W("TRI")], [er])
            mms([(T.B1[:, 16 * mb:256], T.BMW[:], T.EQT[:, mb, 0:256 - 16 * mb], mb == 0, mb == 15, 256 - 16 * mb) for mb in range(lo, lo + 8)],
                [W("BMW"), er], [b1])
        ts(T.FL[:], T.B1[:, 0:256], 0.5, A.is_gt, 256, [b1], [W("FL")])
        mms([(T.B1[:, 256:272], T.EX[:, 15 - i:143 - i], T.FL[:, i:256:16], i == 0, i == 15, 16) for i in range(16)],
            [W("EX"), W("FL")], [("B1", 256, 272)])
        tt(T.DL[:], T.DUP[:], T.LF[:], A.subtract, 32, [W("DUP"), W("LF")], [W("DL")])
        tt(T.OF[:], T.B1[:, 256:272], T.DL[:], A.mult, 32, [("B1", 256, 272), W("DL")], [W("OF")])
        tt(T.OF[:], T.OF[:], T.LF[:], A.add, 32, [W("OF"), W("LF")], [W("OF")])
        cp(T[ol][:], T.OF[:], 16, [W("OF")], [W(ol)])
        scatter("NB0", ov, ol)

    def scatter(nb, ov, ol):
        vec(lambda q: q.tensor_copy(out=T[nb][:, 0:H + DUMMY].indirect(T[ol][:, 0:16]), in_=T[ov][:, 0:256]), 256 * 3,
            [(ov, 0, 256), W(ol)], [(nb, 0, H + DUMMY)])

    def bias(t, a, src):
        c = 4 * (t + 1) + a
        for kb in ("KV", "KW"):
            act(T[kb][:, c:c + 1], T[src][:, 256:257], F.Identity, 1, [(src, 256, 257), (kb, 0, 1)], [(kb, c, c + 1)], bias=T[kb][:, 0:1], scale=32.0)

    def kappa(t):
        ov = "OUTV%d" % t
        mms([(T.B0[:, 0:32], T.ONES[:], T.SPB[:, 0:32], True, True, 32)], [W("ONES"), ("SPB", 0, 32)], [("B0", 0, 32)])
        act(T.JUNK[:], T.B0[:, 0:32], F.Copy, 32, [("B0", 0, 32)], [W("KS1"), W("JUNK")], accum=T.KS1[:, 0:1])
        cp(T.KI[:, 0:1], T.KS1[:, 0:1], 1, [W("KS1")], [W("KI")])
        ts(T.KJ[:, 0:1], T.KI[:, 0:1], 255, A.bitwise_and, 1, [W("KI")], [W("KJ")])
        cp(T[ov][:, 256:257], T.KJ[:, 0:1], 1, [W("KJ")], [(ov, 256, 257)])
        bias(t, 0, ov)

    sent = {}

    def send_update(t):
        dsts = [(rank - a) % NR for a in range(1, NR)]
        ids = [DstId(rid=addr(x)[0], pnc=addr(x)[1]) for x in dsts]
        for nm, inn, sm in (("OUTL%d" % t, "INL%d_%d", "il%d_%d"), ("OUTV%d" % t, "INV%d_%d", "iv%d_%d")):
            def f(q, nm=nm, inn=inn, sm=sm):
                tr = RemoteDMATransfer(dst_ids=ids, dma_engine_mask=emask(cross), remote_sem=T.sem[sm % (rank, t)], srcs=[T[nm][:]],
                                       dsts=[T[inn % (rel(rank, x), t)][:] for x in dsts])
                return q.remote_dma_fused([tr], local_sem=T.sem.lsend)
            num["lsend"] += len(cross)
            bulk.append(add(gr, "G", f, 1.2, [W(nm)], [], "s", "lsend", num["lsend"], soft=bulk[-1:]))
        sent[t] = bulk[-1]

    def apply_update(t, a):
        iv, il = "INV%d_%d" % (a, t), "INL%d_%d" % (a, t)
        src = (rank + a) % NR
        for nm, sm in ((il, "il%d_%d"), (iv, "iv%d_%d")):
            gr["nodes"][add(gr, "R", None, 0.0, [], [W(nm)], "r", sm % (src, t), len(cross), 3.5)]["soft"].add(sent[t])
        bias(t, a, iv)
        scatter("NB%d" % a, iv, il)

    lists(0)
    permute(0)
    gather_headings(0)
    first_v = len(gr["nodes"]) - 1
    lists(1)
    shares(0)
    for t in range(1, RT):
        permute(t)
        load_tiles(t, [first_v])
        shares(t)
    for t in range(RT):
        visits(t)
        election(t)
        if t + 1 < RT:
            headings_out(t)
            notes(t)
            gather_headings(t + 1)
            kappa(t)
            send_update(t)
        else:
            notes(t)
            headings_out(t, [len(gr["nodes"]) - 1])
        write_yh(t)
    for j, e in ((0, "S"), (1, "Y")):
        dma(e, T.yl[:, HALF * j:HALF * j + HALF], T.NB0[:, HALF * j:HALF * j + HALF], 5.0, [("NB0", HALF * j, HALF * j + HALF)], [])
    return gr


def rank_program(g, core, T, topo):
    if T.rank_of(core) is None:
        return
    gr = build(core, T, topo)
    emit_all(gr, schedule(gr), g, T)
